import numpy as np, ml_dtypes
CORES = [36,164,52,180,100,228,116,244]
N = 8
import mx_ref
BF = ml_dtypes.bfloat16
def cols(t, e):
    v = np.concatenate([t.reshape(128, -1, 4), np.zeros((128, 1, 4), BF)], axis=1)
    return np.ascontiguousarray(v[:, e]).reshape(128, -1)
def cut(t, i, w=512):
    return t[:, w * i:w * i + w]
def f(rng, *shape):
    return mx_ref.flush((rng.standard_normal(shape, dtype=np.float32) * np.exp2(rng.integers(-2, 3, shape[:-1] + (1,)))).astype(BF))
def wide(rng, *shape, cols=0):
    v = rng.standard_normal(shape, dtype=np.float32) * np.exp2(rng.integers(-12, 13, shape)).astype(np.float32)
    if cols: v *= np.repeat(np.exp2(rng.integers(-cols, cols + 1, shape[:-2] + (1, shape[-1] // 4))) * (rng.random(shape[:-2] + (1, shape[-1] // 4)) > 0.0625), 4, axis=-1).astype(np.float32)
    return mx_ref.flush(v.astype(BF))
WD, T, PL, CP, NC = 8, 128, 64, 8, 32
def scores(u, x):
    return np.stack([mx_ref.matmul(mx_ref.quantize(u[r]), mx_ref.quantize(x[r]))[0] for r in range(N)])
def fronts(P):
    a = np.zeros(P.shape, bool)
    v, h = P[1:] != P[:-1], P[:, 1:] != P[:, :-1]
    a[1:] |= v; a[:-1] |= v; a[:, 1:] |= h; a[:, :-1] |= h
    return a
def dealt(P):
    i, j = np.nonzero(fronts(P))
    g = np.full((16 * N + 2, WD + 2), -1)
    g[1:-1, 1:-1] = np.arange(N * T).reshape(16 * N, WD)
    n = np.arange(len(i)); D = np.full((N, PL, 5), -1)
    D[(n // 8) % N, 8 * (n // (8 * N)) + n % 8] = np.stack([g[i + 1, j + 1], g[i, j + 1], g[i + 2, j + 1], g[i + 1, j], g[i + 1, j + 2]], axis=1)
    return D
def needed(P):
    return np.stack([np.bincount(e[e >= 0] // T, minlength=N) for e in [np.unique(k) for k in dealt(P)]])
def broken(P):
    if np.sum(fronts(P)) > PL * N: return ["too many active cells"]
    b = []; D = dealt(P)
    for r in range(N):
        c, e = D[r, :, 0], np.unique(D[r])
        if np.bincount(c[c >= 0] // T, minlength=N).max() > CP: b.append("cells of one stripe dealt to one rank")
        if np.bincount(e[e >= 0] // T, minlength=N).max() > NC: b.append("columns of one stripe that one rank needs")
    return b
def smooth(rng, i):
    a, b = np.indices((16 * N, WD)); g = 0
    for _ in range(6):
        t, k, p = rng.uniform(-1, 1), 0.7 * 0.97 ** i * rng.uniform(0.7, 1.4), rng.uniform(0, 6.2832)
        g = g + np.cos(k * (np.cos(t) * a + np.sin(t) * b) + p)
    return g > 0
def straight(rng, i):
    a = np.indices((16 * N, WD))[0]
    return ((a + rng.integers(1, 4)) // 4) % 2 == 0
def islands(rng, i):
    at = [(0, 0), (15, WD // 2)]
    for c in rng.permutation(N * T):
        if len(at) >= int(N * T * 0.0625 * 0.98 ** i): break
        p, q = divmod(int(c), WD)
        if all(abs(p - a) + abs(q - b) >= 3 for a, b in at): at.append((p, q))
    P = np.zeros((16 * N, WD), bool)
    for p, q in at: P[p, q] = True
    return P
def few(rng, i):
    gone = [int(q) for q in 1 + rng.permutation(N - 1)[:rng.integers(1, 3)]]
    if len(gone) == 2 and abs(gone[0] - gone[1]) == 1: gone.pop()
    here = [q for q in range(N) if q not in gone]
    free = [q for q in here if q - 1 not in gone and q + 1 not in gone]
    P = np.zeros((16 * N, WD), bool)
    for q in here:
        if q - 1 in gone: P[16 * q + 1, rng.integers(0, WD)] = True
        if q + 1 in gone: P[16 * q + 14, rng.integers(0, WD)] = True
    for q in free + here[:rng.integers(0, 2)]: P[16 * q + rng.integers(1, 16 if q + 1 in here else 15), rng.integers(0, WD)] = True
    return P
def heavy(rng, i):
    a, b = np.indices((16 * N, WD)); n = np.zeros(a.shape, int); most = rng.integers(0, N)
    low = b % 2 == 1 if WD == 8 else ((b % 2 == 0) & (b > 0)) | (b == WD - 1)
    for r in range(N):
        if r == most:
            for k in (6, 10): n += a >= 16 * r + k + low
            n += a >= 16 * r + 14
            if WD == 8: n[16 * r + 2, 0] += 1
            else: n += a >= 16 * r + 2
        else:
            w = rng.integers(5, 12) + max(0, 3 - 0.1 * i) * np.sin(rng.uniform(0.2, 0.8) * np.arange(WD) + rng.uniform(0, 6.2832))
            n += a >= 16 * r + np.clip(np.rint(w), 2, 14)[None, :]
    return n % 2 == 0
def borders(rng, i):
    a, b = np.indices((16 * N, WD))
    return (a // 16 + (b < rng.integers(1, WD))) % 2 == 0
def drawn(rng, make, uneven=False, idle=False):
    for i in range(50):
        P = make(rng, i) ^ bool(rng.integers(0, 2))
        c = fronts(P).reshape(N, T).sum(axis=1)
        if c.sum() < (1 if idle else 8 * N) or broken(P): continue
        m = needed(P) * (1 - np.eye(N, dtype=int))
        if uneven and (c.max() < 3 * c.min() or m.max() != NC): continue
        if idle and not 1 <= (c == 0).sum() <= 2: continue
        if idle and (c.sum() > 8 * (N - 1) or (c.sum() - 1) % 8 < 3): continue
        if idle and not (m.sum(axis=0)[c == 0] > 0).all(): continue
        return P
    raise RuntimeError("no field in 50 tries")
def sized(t):
    v = t.astype(np.float32)
    return np.where(np.abs(v) < 2.0 ** -30, np.float32(0), v).astype(BF)
def plant(rng, P, spread=False):
    u = sized(f(rng, 128, 512)); qu = mx_ref.quantize(u)
    x = np.zeros((N, 128, T, 4), BF); want = P.reshape(N, T)
    for r in range(N):
        left = np.arange(T)
        for i in range(50):
            k = len(left); m = 8 * -(-k // 8)
            t = sized(wide(rng, 128, 4 * m, cols=2) if spread else f(rng, 128, 4 * m))
            s = mx_ref.matmul(qu, mx_ref.quantize(t))[0][:k]
            turn = np.where((s > 0) == want[r, left], 1, -1)
            t = (t.astype(np.float32).reshape(128, m, 4)[:, :k] * turn[None, :, None]).astype(BF)
            ok = np.abs(s) > 32
            x[r][:, left[ok]] = t[:, ok]
            left = left[~ok]
            if len(left) == 0: break
        else: raise RuntimeError("scores too small in 50 tries")
    return {"x": x.reshape(N, 128, 4 * T), "u": np.stack([u] * N), "w": sized(f(rng, N, 128, 5120))}
def setup_inputs(rng):
    return plant(rng, drawn(rng, smooth))
def setup_inputs_few(rng):
    return plant(rng, drawn(rng, few, idle=True))
def setup_inputs_near(rng):
    for i in range(50):
        d = plant(rng, drawn(rng, borders))
        s = scores(d["u"], d["x"])
        e = 1 + int(np.floor(np.log2(float(np.abs(s).min()))))
        d["u"] = sized((d["u"].astype(np.float32) * np.float32(2.0 ** -e)).astype(BF))
        t = scores(d["u"], d["x"])
        if 0.5 < np.abs(t).min() <= 1 and np.array_equal(t > 0, s > 0): return d
    raise RuntimeError("no scores near 0.5 in 50 tries")
def setup_inputs_spread(rng):
    return plant(rng, drawn(rng, islands), spread=True)
def setup_inputs_straight(rng):
    return plant(rng, drawn(rng, straight))
def setup_inputs_uneven(rng):
    return plant(rng, drawn(rng, heavy, uneven=True))
def check_inputs(d):
    b = []
    for k in ("x", "u", "w"):
        v = np.abs(d[k].astype(np.float32))
        if not ((v == 0) | ((v >= 2.0 ** -30) & (v <= 2.0 ** 30))).all(): b.append("sizes of " + k)
    if b: return b
    for r in range(N):
        if not np.array_equal(d["u"][r].astype(np.float32), d["u"][0].astype(np.float32)): b.append("u")
    s = scores(d["u"], d["x"])
    if not (np.abs(s) > 0.5).all(): b.append("score")
    return b + broken((s > 0).reshape(16 * N, WD))
def reference(x, u, w):
    P = (scores(u, x) > 0).reshape(16 * N, WD)
    D = dealt(P)
    m = max(8, 8 * -(-int(np.sum(fronts(P))) // (8 * N)))
    X = np.concatenate(list(x), axis=1)
    y = np.zeros((N, 128, 2 * PL), np.float32)
    for r in range(N):
        for k in range(5):
            q = mx_ref.quantize(cols(X, D[r, :m, k]))
            for o in range(2): y[r][:, PL * o:PL * o + m] += mx_ref.matmul(mx_ref.quantize(cut(w[r], 2 * k + o)), q)
    return {"y": y}

@@ -1,0 +1,332 @@
+from concourse.bass import DstId, RemoteDMATransfer
+from concourse.mybir import dt, AluOpType, AxisListType, ActivationFunctionType
+
+A = AluOpType
+F = ActivationFunctionType
+C4, U8 = "float8_e4m3fn_x4", "uint8"
+BF, F32 = "bfloat16", "float32"
+HUGE = 1e29
+BIG = 1.5 * 2.0 ** 30
+SCRATCH = {
+    "xs": ("sbuf", [128, 512], BF), "us": ("sbuf", [128, 4], BF), "ut": ("sbuf", [128, 512], BF),
+    "ln": ("sbuf", [128, 512], BF), "rn": ("sbuf", [128, 512], BF), "zt": ("sbuf", [128, 512], BF),
+    "wt": ("sbuf", [128, 5120], BF),
+    "qu": ("sbuf", [128, 128], C4), "su": ("sbuf", [128, 128], U8),
+    "qx": ("sbuf", [128, 128], C4), "sx": ("sbuf", [128, 128], U8),
+    "wx": ("sbuf", [128, 416], C4), "swx": ("sbuf", [128, 416], U8),
+    "slot": ("sbuf", [128, 384], C4), "sslot": ("sbuf", [128, 384], U8),
+    "land": ("sbuf", [128, 512], C4), "sland": ("sbuf", [128, 512], U8),
+    "mv": ("sbuf", [128, 448], C4), "smv": ("sbuf", [128, 448], U8),
+    "qw": ("sbuf", [128, 1280], C4), "sw": ("sbuf", [128, 1280], U8),
+    "sg": ("sbuf", [128, 128], BF), "pq": ("sbuf", [128, 512], BF), "ctl": ("sbuf", [128, 512], BF),
+    "a4": ("sbuf", [128, 512], BF), "nn": ("sbuf", [128, 128], BF), "j1": ("sbuf", [128, 128], BF),
+    "j2": ("sbuf", [128, 128], BF), "j3": ("sbuf", [128, 128], BF),
+    "acc": ("sbuf", [128, 2], F32), "base": ("sbuf", [128, 128], BF), "po": ("sbuf", [128, 128], BF),
+    "mg": ("sbuf", [128, 8, 40], BF), "pr": ("sbuf", [128, 112], BF), "cc": ("sbuf", [128, 8], F32),
+    "cs": ("sbuf", [128, 112], F32), "aq": ("sbuf", [128, 8], F32), "rr": ("sbuf", [128, 128], BF),
+    "pi": ("sbuf", [128, 1], "int32"), "e5": ("sbuf", [128, 1], "int32"), "hi": ("sbuf", [128, 1], "int32"),
+    "s7": ("sbuf", [128, 1], "int32"), "mi": ("sbuf", [128, 32], "int32"), "mj": ("sbuf", [128, 32], "int32"),
+    "rs0": ("sbuf", [128, 64], F32), "rs": ("sbuf", [128, 64], F32),
+    "c63": ("sbuf", [128, 2], F32), "c1": ("sbuf", [128, 2], F32), "mh": ("sbuf", [128, 32], F32),
+    "m1": ("sbuf", [128, 32], F32), "kk": ("sbuf", [128, 3], F32),
+    "tb": ("sbuf", [128, 2], F32), "tw": ("sbuf", [128, 2], F32), "thr": ("sbuf", [128, 2], F32),
+    "cm": ("sbuf", [128, 128], BF), "acl": ("sbuf", [128, 1], F32), "cl1": ("sbuf", [128, 1], F32),
+    "it": ("sbuf", [128, 64], F32), "tt": ("sbuf", [128, 64], F32), "ss": ("sbuf", [128, 64], F32),
+    "off": ("sbuf", [128, 24], "uint16"), "offo": ("sbuf", [128, 4], "uint16"),
+    "n0": ("sbuf", [128, 4], F32), "n2": ("sbuf", [128, 4], F32), "hs": ("sbuf", [128, 2], F32),
+    "kr0": ("sbuf", [128, 5], F32), "kr": ("sbuf", [128, 5], F32), "cq": ("sbuf", [128, 32], F32),
+    "sq": ("sbuf", [128, 32], F32), "offr": ("sbuf", [128, 20], "uint16"),
+    "yo": ("sbuf", [128, 128], F32),
+    "sc": ("psum", [128, 512], F32), "ps": ("psum", [128, 1024], F32),
+}
+SEMAPHORES = ["v", "du", "dx", "dl", "dw0", "dw1", "gi", "gm", "eu", "eq", "pm", "esg", "s1", "s2", "ea", "em",
+              "eth", "sa", "et", "eo", "ep", "es", "eo2", "ep2", "es2", "ew", "er", "py0", "py1", "yv", "ys", "dy",
+              "halo", "msg", "cod", "loc"] + ["kv%d" % k for k in range(5)] + ["ks%d" % k for k in range(5)]
+
+
+def rank_program(g, core, T, topo):
+    r = T.rank_of(core)
+    if r is None:
+        return
+    N = len(T.cores)
+    V, S, Y, P = g.vector, g.scalar, g.sync, g.tensor
+    cnt = {}
+
+    def inc(i, name, k=1):
+        i.then_inc(T.sem[name], k)
+        cnt[name] = cnt.get(name, 0) + k
+
+    def wait(q, name):
+        q.wait_ge(T.sem[name], cnt[name])
+
+    def v(i):
+        inc(i, "v")
+
+    def vw():
+        wait(V, "v")
+
+    def to(d):
+        rid, pnc = topo.addr(T.cores[d], core)
+        return DstId(rid=rid, pnc=pnc)
+
+    def engs(d):
+        return topo.engines(core, T.cores[d])
+
+    def mask(es):
+        return int(sum(1 << e for e in es))
+
+    others = [d for d in range(N) if d != r]
+    near = [d for d in (r - 1, r + 1) if 0 <= d < N]
+
+    inc(S.dma_start(T.us[:], T.u[:, 0:4]), "du", 16)
+    inc(Y.dma_start(T.xs[:], T.x[:]), "dx", 16)
+    inc(S.dma_start(T.ln[:, 4:512], T.x[:, 0:508]), "dl", 16)
+    inc(S.dma_start(T.rn[:, 0:508], T.x[:, 4:512]), "dl", 16)
+    inc(Y.dma_start(T.wt[:, 0:2560], T.w[:, 0:2560]), "dw0", 16)
+
+    inc(g.iota(T.pi[:], [[1, 1]], 0, 1), "gi")
+    inc(g.iota(T.mi[:], [[1, 32]], 256, -1), "gi")
+    inc(g.iota(T.rs0[:], [[0, 8], [1, 8]], 0, 0, allow_small_or_imprecise_dtypes=True), "gi")
+    inc(g.iota(T.n0[:], [[256, 4]], 16 * r, 0, allow_small_or_imprecise_dtypes=True), "gi")
+    inc(g.iota(T.kr0[:], [[8, 5]], 0, 0, allow_small_or_imprecise_dtypes=True), "gi")
+    v(V.memset(T.zt[:], 0.0))
+    v(V.memset(T.pq[:], 1.0))
+    v(V.memset(T.ctl[:], -HUGE))
+    vw()
+    v(V.memset(T.ctl[:, 0:512:4], HUGE))
+    v(V.memset(T.po[:], 0.0))
+    wait(V, "gi")
+    v(V.tensor_scalar(T.e5[:], T.pi[:], 31, None, A.bitwise_and))
+    v(V.tensor_scalar(T.hi[:], T.pi[:], 3, 1, A.logical_shift_right, A.bitwise_and))
+    v(V.tensor_scalar(T.s7[:], T.pi[:], 7, None, A.bitwise_and))
+    v(V.tensor_scalar(T.mj[:], T.mi[:], 7, None, A.bitwise_and))
+    v(V.tensor_scalar(T.rs[:], T.rs0[:], 0.5, None, A.is_gt))
+    vw()
+
+    wait(V, "du")
+    for t in range(4):
+        v(V.tensor_scalar(T.ut[:, t:512:4], T.zt[:, 0:128], T.us[:, t:t + 1], None, A.add))
+    vw()
+    inc(V.quantize_mx(T.qu[:], T.su[:], T.ut[:]), "eu")
+    wait(V, "dx")
+    inc(V.quantize_mx(T.qx[:], T.sx[:], T.xs[:]), "eq")
+    wait(P, "eu")
+    wait(P, "eq")
+    inc(P.matmul_mx(T.sc[:, 0:128], T.qu[:], T.su[:], T.qx[:], T.sx[:], True, True), "pm")
+
+    wait(g, "eq")
+    part = {d: [e for i, e in enumerate(engs(d)) if i // (len(engs(d)) // len(near)) == near.index(d)] for d in near}
+    for plane in (0, 1):
+        tr = []
+        for d in near:
+            a, b = (120, 8) if d > r else (0, 144)
+            if plane:
+                src, dst = T.sx[:, a:a + 8], T.swx[:, b:b + 8]
+            else:
+                src, dst = T.qx[:, a:a + 8].bitcast(dt.uint8), T.wx[:, b:b + 8].bitcast(dt.uint8)
+            tr.append(RemoteDMATransfer(dst_ids=[to(d)], dma_engine_mask=mask(part[d]), remote_sem=T.sem.halo,
+                                        src=src, dst=dst))
+        g.remote_dma_fused(tr, local_sem=T.sem.loc)
+    halo = 0
+    for d in near:
+        nd = len([x for x in (d - 1, d + 1) if 0 <= x < N])
+        halo += 2 * (len(topo.engines(T.cores[d], core)) // nd)
+
+    wait(V, "pm")
+    inc(V.tensor_scalar(T.sg[:], T.sc[:, 0:128], -0.5, 0.5, A.max, A.min), "esg")
+    wait(S, "esg")
+    inc(S.activation(T.mg[:, r, 0:8], T.sg[:, 0:8], F.Copy), "s1")
+    inc(S.activation(T.mg[:, r, 26:34], T.sg[:, 120:128], F.Copy), "s1")
+    wait(V, "esg")
+    v(V.tensor_tensor(T.pq[:, 0:505:4], T.sg[:, 0:127], T.sc[:, 1:128], A.mult))
+    v(V.tensor_tensor(T.pq[:, 5:510:4], T.sg[:, 1:128], T.sc[:, 0:127], A.mult))
+    v(V.tensor_tensor(T.pq[:, 2:479:4], T.sg[:, 0:120], T.sc[:, 8:128], A.mult))
+    v(V.tensor_tensor(T.pq[:, 35:512:4], T.sg[:, 8:128], T.sc[:, 0:120], A.mult))
+    vw()
+    v(V.memset(T.pq[:, 28:512:32], 1.0))
+    v(V.memset(T.pq[:, 1:512:32], 1.0))
+    vw()
+    inc(V.tensor_tensor_scan(T.a4[:], T.ctl[:], T.pq[:], 0.0, A.max, A.min), "ea")
+
+    l1 = 120 if r < N - 1 else 128
+    l2 = 8 if r > 0 else 0
+    bias = (256 - (l1 + 128 - l2) / 2) / 2
+    wait(S, "ea")
+    inc(S.activation(T.j1[:, 0:l1], T.a4[:, 3:4 * l1:4], F.Sign, scale=-1.0, accum_out=T.acc[:, 0:1]), "s2")
+    inc(S.activation(T.j2[:, 0:128 - l2], T.a4[:, 3 + 4 * l2:512:4], F.Sign, scale=-1.0,
+                     accum_out=T.acc[:, 1:2]), "s2")
+    wait(S, "s2")
+    inc(S.activation(T.mg[:, r, 16:18], T.acc[:], F.Identity, bias=float(bias), scale=0.5), "s1")
+    wait(V, "ea")
+    v(V.tensor_scalar(T.nn[:], T.a4[:, 3:512:4], 0.0, -4.0, A.is_gt, A.mult))
+    vw()
+    inc(V.tensor_tensor(T.mg[:, r, 8:16], T.nn[:, 0:8], T.sg[:, 0:8], A.mult), "em")
+    inc(V.tensor_tensor(T.mg[:, r, 18:26], T.nn[:, 120:128], T.sg[:, 120:128], A.mult), "em")
+    m0, m1 = (16 if r == 0 else 0), (18 if r == N - 1 else 34)
+    wait(g, "em")
+    wait(g, "s1")
+    g.remote_dma_fused([RemoteDMATransfer(dst_ids=[to(d) for d in others], dma_engine_mask=mask(engs(others[0])),
+                                          remote_sem=T.sem.msg, srcs=[T.mg[:, r, m0:m1]],
+                                          dsts=[T.mg[:, r, m0:m1] for d in others])], local_sem=T.sem.loc)
+    g.sem_inc(T.sem.gm, 1)
+    Y.wait_ge(T.sem.gm, 1)
+    inc(Y.dma_start(T.wt[:, 2560:5120], T.w[:, 2560:5120]), "dw1", 16)
+    msg = sum(len(topo.engines(T.cores[d], core)) for d in others)
+
+    v(V.tensor_scalar(T.base[:, 8:120], T.nn[:, 8:120], 0.5, 2.0, A.mult, A.add))
+    v(V.tensor_scalar(T.base[:, 0:8], T.nn[:, 0:8], 0.25 if r > 0 else 0.5, 2.0, A.mult, A.add))
+    v(V.tensor_scalar(T.base[:, 120:128], T.nn[:, 120:128], 0.25 if r < N - 1 else 0.5, 2.0, A.mult, A.add))
+    for m in (0, 1):
+        v(V.tensor_scalar(T.c63[:, m:m + 1], T.e5[:], -2.0, 63.0 - 64.0 * m, A.mult, A.add))
+        v(V.tensor_scalar(T.c1[:, m:m + 1], T.e5[:], 2.0, 64.0 * m + 1.0, A.mult, A.add))
+    v(V.tensor_scalar(T.mh[:], T.mj[:], 0.0, 0.5, A.is_equal, A.mult))
+    v(V.tensor_scalar(T.m1[:], T.mj[:], 0.0, None, A.is_equal))
+    v(V.tensor_scalar(T.kk[:, 0:1], T.hi[:], -8.0, 80.0, A.mult, A.add))
+    v(V.tensor_scalar(T.kk[:, 1:2], T.hi[:], 136.0, 88.0, A.mult, A.add))
+    v(V.tensor_scalar(T.kk[:, 2:3], T.hi[:], 0.0, 352.0, A.mult, A.add))
+    if r == 0:
+        v(V.quantize_mx(T.wx[:, 8:136], T.swx[:, 8:136], T.zt[:]))
+    if r == N - 1:
+        v(V.quantize_mx(T.wx[:, 24:152], T.swx[:, 24:152], T.zt[:]))
+    wait(V, "dl")
+    for t in range(4):
+        v(V.memset(T.ln[:, t:512:32], 0.0))
+        v(V.memset(T.rn[:, 28 + t:512:32], 0.0))
+    vw()
+    v(V.quantize_mx(T.wx[:, 16:144], T.swx[:, 16:144], T.xs[:]))
+    v(V.quantize_mx(T.wx[:, 160:288], T.swx[:, 160:288], T.ln[:]))
+    v(V.quantize_mx(T.wx[:, 288:416], T.swx[:, 288:416], T.rn[:]))
+    vw()
+
+    V.wait_ge(T.sem.msg, msg)
+    wait(V, "s1")
+    wait(V, "em")
+    if r > 0:
+        v(V.tensor_tensor(T.po[:, 0:8], T.mg[:, r, 8:16], T.mg[:, r - 1, 26:34], A.mult))
+    if r < N - 1:
+        v(V.tensor_tensor(T.po[:, 120:128], T.mg[:, r, 18:26], T.mg[:, r + 1, 0:8], A.mult))
+    v(V.tensor_tensor_scan(T.cc[:], T.mg[:, :, 16], T.mg[:, :, 17], 0.0, A.add, A.add))
+    v(V.tensor_tensor(T.pr[:], T.mg[:, 0:N - 1, 18:34], T.mg[:, 1:N, 0:16], A.mult))
+    vw()
+    v(V.tensor_tensor_scan(T.cs[:], T.zt[:, 0:112], T.pr[:], T.cc[:, r - 1:r] if r > 0 else 0.0, A.add, A.add))
+    v(V.tensor_tensor_scan(T.rr[:], T.base[:], T.po[:], 0.0, A.add, A.add))
+    vw()
+    if r == 0:
+        inc(V.tensor_copy(T.thr[:], T.c1[:]), "eth")
+    else:
+        a2 = T.cs[:, 16 * r - 9:16 * r - 8]
+        v(V.tensor_scalar(T.tb[:], T.c63[:], a2, BIG, A.add, A.add))
+        v(V.tensor_scalar(T.tw[:], T.c1[:], a2, None, A.subtract))
+        vw()
+        inc(V.tensor_scalar(T.thr[:, 0:1], T.tb[:, 0:1], BIG, T.tw[:, 0:1], A.subtract, A.add), "eth")
+        v(V.tensor_scalar(T.thr[:, 1:2], T.tb[:, 1:2], BIG, T.tw[:, 1:2], A.subtract, A.add))
+    wait(S, "eth")
+    inc(S.activation(T.j3[:], T.rr[:], F.Sign, bias=T.thr[:, 0:1], scale=-1.0, accum_out=T.acl[:]), "sa")
+    wait(S, "sa")
+    inc(S.activation(T.it[:, 0:32], T.mh[:], F.Copy, scale=T.acl[:]), "et")
+    vw()
+    wait(V, "eth")
+    v(V.tensor_scalar(T.cm[:], T.rr[:], T.thr[:, 1:2], 0.5, A.is_le, A.subtract))
+    vw()
+    v(V.tensor_reduce(T.cl1[:], T.cm[:], AxisListType.X, A.add))
+    vw()
+    v(V.tensor_scalar(T.it[:, 32:64], T.m1[:], T.cl1[:], None, A.mult))
+    vw()
+    wait(V, "et")
+    v(V.transpose(T.tt[:], T.it[:]))
+    vw()
+    v(V.tensor_tensor_scan(T.ss[:], T.rs[:], T.tt[:], 0.0, A.mult, A.add))
+    vw()
+    for k in range(3):
+        inc(V.tensor_scalar(T.off[:, k:24:3], T.ss[:, 7:64:8], 63.0, T.kk[:, k:k + 1], A.min, A.add), "eo")
+    wait(V, "eo")
+    V.wait_ge(T.sem.halo, halo)
+    inc(V.tensor_copy(T.slot[:].bitcast(dt.uint32), T.wx[:].bitcast(dt.uint32).indirect(T.off[:])), "ep")
+    wait(S, "eo")
+    S.wait_ge(T.sem.halo, halo)
+    inc(S.activation(T.sslot[:], T.swx[:].indirect(T.off[:]), F.Copy), "es")
+
+    for plane in (0, 1):
+        wait(g, "es" if plane else "ep")
+        tr = []
+        for i, d in enumerate(others):
+            if plane:
+                src, dst = T.sslot[:, 48 * d:48 * d + 40], T.sland[:, 48 * r:48 * r + 40]
+            else:
+                src = T.slot[:, 48 * d:48 * d + 40].bitcast(dt.uint8)
+                dst = T.land[:, 48 * r:48 * r + 40].bitcast(dt.uint8)
+            tr.append(RemoteDMATransfer(dst_ids=[to(d)], dma_engine_mask=mask([engs(d)[i]]), remote_sem=T.sem.cod,
+                                        src=src, dst=dst))
+        g.remote_dma_fused(tr, local_sem=T.sem.loc)
+
+    for k in range(3):
+        inc(V.tensor_scalar(T.offo[:, k:k + 1], T.ss[:, 8 * r + 7:8 * r + 8], 63.0, T.kk[:, k:k + 1],
+                            A.min, A.add), "eo2")
+    wait(V, "eo2")
+    inc(V.tensor_copy(T.land[:, 48 * r:48 * r + 48].bitcast(dt.uint32),
+                      T.wx[:].bitcast(dt.uint32).indirect(T.offo[:, 0:3])), "ep2")
+    wait(S, "eo2")
+    inc(S.activation(T.sland[:, 48 * r:48 * r + 48], T.swx[:].indirect(T.offo[:, 0:3]), F.Copy), "es2")
+
+    v(V.quantize_mx(T.land[:, 384:512], T.sland[:, 384:512], T.zt[:]))
+    v(V.quantize_mx(T.mv[:, 320:448], T.smv[:, 320:448], T.zt[:]))
+
+    v(V.tensor_scalar(T.hs[:, 0:1], T.s7[:], 1.0, None, A.mult))
+    v(V.tensor_scalar(T.hs[:, 1:2], T.hi[:], 128.0, None, A.mult))
+    v(V.tensor_tensor(T.aq[:, 0:7], T.cc[:, 0:7], T.cs[:, 7:112:16], A.add))
+    v(V.tensor_tensor(T.aq[:, 7:8], T.cc[:, 7:8], T.cs[:, 111:112], A.add))
+    vw()
+    v(V.tensor_scalar(T.kr[:], T.kr0[:], T.hs[:, 0:1], None, A.add))
+    v(V.tensor_scalar(T.n2[:], T.n0[:], T.hs[:, 0:1], T.hs[:, 1:2], A.add, A.add))
+    vw()
+    if r > 0:
+        v(V.tensor_scalar(T.n2[:], T.n2[:], T.hs[:, 0:1], T.cc[:, r - 1:r], A.add, A.add))
+    else:
+        v(V.tensor_scalar(T.n2[:], T.n2[:], T.hs[:, 0:1], None, A.add))
+    vw()
+    for c in range(4):
+        v(V.tensor_scalar(T.cq[:, 8 * c:8 * c + 8], T.aq[:], T.n2[:, c:c + 1], 48.0, A.is_le, A.mult))
+    vw()
+    v(V.tensor_tensor_scan(T.sq[:], T.rs[:, 0:32], T.cq[:], 0.0, A.mult, A.add))
+    vw()
+    for k in range(5):
+        inc(V.tensor_scalar(T.offr[:, 4 * k:4 * k + 4], T.sq[:, 7:32:8], T.kr[:, k:k + 1], None, A.add), "er")
+
+    wait(V, "dw0")
+    inc(V.quantize_mx(T.qw[:, 0:512], T.sw[:, 0:512], T.wt[:, 0:2048]), "ew")
+    wait(V, "dw1")
+    inc(V.quantize_mx(T.qw[:, 512:1024], T.sw[:, 512:1024], T.wt[:, 2048:4096]), "ew")
+    inc(V.quantize_mx(T.qw[:, 1024:1280], T.sw[:, 1024:1280], T.wt[:, 4096:5120]), "ew")
+
+    for q in (V, S):
+        wait(q, "er")
+        wait(q, "ep2")
+        wait(q, "es2")
+        q.wait_ge(T.sem.cod, 2 * len(others))
+    wait(P, "ew")
+    for k in range(5):
+        o16 = T.offr[:, 4 * k:4 * k + 4]
+        inc(V.tensor_copy(T.mv[:, 64 * k:64 * k + 64].bitcast(dt.uint32),
+                          T.land[:].bitcast(dt.uint32).indirect(o16)), "kv%d" % k)
+        inc(S.activation(T.smv[:, 64 * k:64 * k + 64], T.sland[:].indirect(o16), F.Copy), "ks%d" % k)
+    for k in range(5):
+        for kk in ([0, 1] if k == 0 else [k + 1] if k < 4 else []):
+            wait(P, "kv%d" % kk)
+            wait(P, "ks%d" % kk)
+        for o in (0, 1):
+            w0 = 128 * (2 * k + o)
+            i = P.matmul_mx(T.ps[:, 512 * o:512 * o + 128], T.qw[:, w0:w0 + 128], T.sw[:, w0:w0 + 128],
+                            T.mv[:, 64 * k:64 * k + 128], T.smv[:, 64 * k:64 * k + 128], k == 0, k == 4)
+            if k == 4:
+                inc(i, "py%d" % o)
+    wait(V, "py0")
+    inc(V.tensor_copy(T.yo[:, 0:64], T.ps[:, 0:64]), "yv")
+    wait(Y, "yv")
+    inc(Y.dma_start(T.y[:, 0:64], T.yo[:, 0:64]), "dy", 16)
+    wait(S, "py1")
+    inc(S.activation(T.yo[:, 64:128], T.ps[:, 512:576], F.Copy), "ys")
+    wait(S, "ys")
+    inc(S.dma_start(T.y[:, 64:128], T.yo[:, 64:128]), "dy", 16)
+    wait(Y, "dy")
+    vw()
+    g.wait_ge(T.sem.loc, 3 * len(engs(others[0])) + 2 * len(others))

@@ -6,7 +6,8 @@ F = ActivationFunctionType
 C4, U8 = "float8_e4m3fn_x4", "uint8"
 BF, F32 = "bfloat16", "float32"
 HUGE = 1e29
-BIG = 1.5 * 2.0 ** 30
+BIG = 1.5 * 2.0 ** 32
+ST = 40
 SCRATCH = {
     "xs": ("sbuf", [128, 512], BF), "us": ("sbuf", [128, 4], BF), "ut": ("sbuf", [128, 512], BF),
     "ln": ("sbuf", [128, 512], BF), "rn": ("sbuf", [128, 512], BF), "zt": ("sbuf", [128, 512], BF),
@@ -14,33 +15,37 @@ SCRATCH = {
     "qu": ("sbuf", [128, 128], C4), "su": ("sbuf", [128, 128], U8),
     "qx": ("sbuf", [128, 128], C4), "sx": ("sbuf", [128, 128], U8),
     "wx": ("sbuf", [128, 416], C4), "swx": ("sbuf", [128, 416], U8),
-    "slot": ("sbuf", [128, 384], C4), "sslot": ("sbuf", [128, 384], U8),
+    "slota": ("sbuf", [128, 192], C4), "sslota": ("sbuf", [128, 192], U8),
+    "slotb": ("sbuf", [128, 192], C4), "sslotb": ("sbuf", [128, 192], U8),
     "land": ("sbuf", [128, 512], C4), "sland": ("sbuf", [128, 512], U8),
     "mv": ("sbuf", [128, 448], C4), "smv": ("sbuf", [128, 448], U8),
     "qw": ("sbuf", [128, 1280], C4), "sw": ("sbuf", [128, 1280], U8),
-    "sg": ("sbuf", [128, 128], BF), "pq": ("sbuf", [128, 512], BF), "ctl": ("sbuf", [128, 512], BF),
-    "a4": ("sbuf", [128, 512], BF), "nn": ("sbuf", [128, 128], BF), "j1": ("sbuf", [128, 128], BF),
-    "j2": ("sbuf", [128, 128], BF), "j3": ("sbuf", [128, 128], BF),
-    "acc": ("sbuf", [128, 2], F32), "base": ("sbuf", [128, 128], BF), "po": ("sbuf", [128, 128], BF),
-    "mg": ("sbuf", [128, 8, 40], BF), "pr": ("sbuf", [128, 112], BF), "cc": ("sbuf", [128, 8], F32),
-    "cs": ("sbuf", [128, 112], F32), "aq": ("sbuf", [128, 8], F32), "rr": ("sbuf", [128, 128], BF),
-    "pi": ("sbuf", [128, 1], "int32"), "e5": ("sbuf", [128, 1], "int32"), "hi": ("sbuf", [128, 1], "int32"),
-    "s7": ("sbuf", [128, 1], "int32"), "mi": ("sbuf", [128, 32], "int32"), "mj": ("sbuf", [128, 32], "int32"),
+    "sgp": ("sbuf", [128, 18, 10], BF), "pq": ("sbuf", [128, 512], BF), "ctl": ("sbuf", [128, 512], BF),
+    "a4": ("sbuf", [128, 512], BF), "nnp": ("sbuf", [128, 144], BF),
+    "mo": ("sbuf", [128, ST * 128], BF), "mg": ("sbuf", [128, 8, 40], BF), "jr": ("sbuf", [128, 8], F32),
+    "cr": ("sbuf", [128, 1], F32), "j3": ("sbuf", [128, 128], F32),
+    "base": ("sbuf", [128, 128], BF), "po": ("sbuf", [128, 128], BF), "pr": ("sbuf", [128, 120], BF),
+    "cc": ("sbuf", [128, 8], F32), "cs": ("sbuf", [128, 120], F32), "aq": ("sbuf", [128, 8], F32),
+    "rr": ("sbuf", [128, 128], BF),
+    "pi": ("sbuf", [128, 1], "int32"), "ci": ("sbuf", [128, 3], "int32"), "cf": ("sbuf", [128, 3], F32),
+    "mi": ("sbuf", [128, 32], "int32"), "mj": ("sbuf", [128, 32], "int32"), "i2": ("sbuf", [128, 2], F32),
     "rs0": ("sbuf", [128, 64], F32), "rs": ("sbuf", [128, 64], F32),
     "c63": ("sbuf", [128, 2], F32), "c1": ("sbuf", [128, 2], F32), "mh": ("sbuf", [128, 32], F32),
-    "m1": ("sbuf", [128, 32], F32), "kk": ("sbuf", [128, 3], F32),
+    "m1": ("sbuf", [128, 32], F32), "kk": ("sbuf", [128, 2], F32), "hs": ("sbuf", [128, 1], F32),
     "tb": ("sbuf", [128, 2], F32), "tw": ("sbuf", [128, 2], F32), "thr": ("sbuf", [128, 2], F32),
     "cm": ("sbuf", [128, 128], BF), "acl": ("sbuf", [128, 1], F32), "cl1": ("sbuf", [128, 1], F32),
     "it": ("sbuf", [128, 64], F32), "tt": ("sbuf", [128, 64], F32), "ss": ("sbuf", [128, 64], F32),
-    "off": ("sbuf", [128, 24], "uint16"), "offo": ("sbuf", [128, 4], "uint16"),
-    "n0": ("sbuf", [128, 4], F32), "n2": ("sbuf", [128, 4], F32), "hs": ("sbuf", [128, 2], F32),
+    "offa": ("sbuf", [128, 12], "uint16"), "offb": ("sbuf", [128, 12], "uint16"),
+    "offo": ("sbuf", [128, 4], "uint16"),
+    "n0": ("sbuf", [128, 4], F32), "n2": ("sbuf", [128, 4], F32),
     "kr0": ("sbuf", [128, 5], F32), "kr": ("sbuf", [128, 5], F32), "cq": ("sbuf", [128, 32], F32),
     "sq": ("sbuf", [128, 32], F32), "offr": ("sbuf", [128, 20], "uint16"),
     "yo": ("sbuf", [128, 128], F32),
     "sc": ("psum", [128, 512], F32), "ps": ("psum", [128, 1024], F32),
 }
-SEMAPHORES = ["v", "du", "dx", "dl", "dw0", "dw1", "gi", "gm", "eu", "eq", "pm", "esg", "s1", "s2", "ea", "em",
-              "eth", "sa", "et", "eo", "ep", "es", "eo2", "ep2", "es2", "ew", "er", "py0", "py1", "yv", "ys", "dy",
+SEMAPHORES = ["v", "z", "du", "dx", "dl", "dw0", "dw1", "gi", "gi2", "gi3", "eu", "eq", "pm", "esg", "s1", "ea", "em",
+              "so", "sz", "ec", "sk", "sk2", "ecr", "eth", "err", "sa", "et", "eoa", "epa", "esa", "eob", "epb", "esb",
+              "eo2", "ep2", "es2", "ew", "er", "py0", "py1", "yv", "ys", "dy",
               "halo", "msg", "cod", "loc"] + ["kv%d" % k for k in range(5)] + ["ks%d" % k for k in range(5)]
 
 
@@ -69,8 +74,8 @@ def rank_program(g, core, T, topo):
         rid, pnc = topo.addr(T.cores[d], core)
         return DstId(rid=rid, pnc=pnc)
 
-    def engs(d):
-        return topo.engines(core, T.cores[d])
+    def engs(d, s=r):
+        return topo.engines(T.cores[s], T.cores[d])
 
     def mask(es):
         return int(sum(1 << e for e in es))
@@ -78,31 +83,39 @@ def rank_program(g, core, T, topo):
     others = [d for d in range(N) if d != r]
     near = [d for d in (r - 1, r + 1) if 0 <= d < N]
 
+    def batch(s, b):
+        return [(s + j) % N for j in range(1, N) if j % 2 == 1 - b]
+
+    def deal(s, b, plane):
+        ds = batch(s, b)
+        es = engs(ds[0], s)
+        n = len(es) // 4
+        w = [1] * 4 if len(ds) == 4 else [2, 1, 1] if plane else [1, 1, 2]
+        out, at = {}, 0
+        for d, k in zip(ds, w):
+            out[d] = es[at:at + n * k]
+            at += n * k
+        return out
+
     inc(S.dma_start(T.us[:], T.u[:, 0:4]), "du", 16)
     inc(Y.dma_start(T.xs[:], T.x[:]), "dx", 16)
     inc(S.dma_start(T.ln[:, 4:512], T.x[:, 0:508]), "dl", 16)
-    inc(S.dma_start(T.rn[:, 0:508], T.x[:, 4:512]), "dl", 16)
+    inc(Y.dma_start(T.rn[:, 0:508], T.x[:, 4:512]), "dl", 16)
     inc(Y.dma_start(T.wt[:, 0:2560], T.w[:, 0:2560]), "dw0", 16)
+    inc(Y.dma_start(T.wt[:, 2560:5120], T.w[:, 2560:5120]), "dw1", 16)
 
-    inc(g.iota(T.pi[:], [[1, 1]], 0, 1), "gi")
+    inc(g.iota(T.pi[:], [[1, 1]], 0, 8), "gi")
     inc(g.iota(T.mi[:], [[1, 32]], 256, -1), "gi")
     inc(g.iota(T.rs0[:], [[0, 8], [1, 8]], 0, 0, allow_small_or_imprecise_dtypes=True), "gi")
-    inc(g.iota(T.n0[:], [[256, 4]], 16 * r, 0, allow_small_or_imprecise_dtypes=True), "gi")
-    inc(g.iota(T.kr0[:], [[8, 5]], 0, 0, allow_small_or_imprecise_dtypes=True), "gi")
-    v(V.memset(T.zt[:], 0.0))
-    v(V.memset(T.pq[:], 1.0))
+    inc(g.iota(T.i2[:], [[256, 2]], 4, 0, allow_small_or_imprecise_dtypes=True), "gi2")
+    inc(V.memset(T.zt[:, 0:128], 0.0), "z")
     v(V.memset(T.ctl[:], -HUGE))
+    v(V.memset(T.sgp[:], 0.0))
+    v(V.memset(T.nnp[:], 0.0))
     vw()
     v(V.memset(T.ctl[:, 0:512:4], HUGE))
-    v(V.memset(T.po[:], 0.0))
-    wait(V, "gi")
-    v(V.tensor_scalar(T.e5[:], T.pi[:], 31, None, A.bitwise_and))
-    v(V.tensor_scalar(T.hi[:], T.pi[:], 3, 1, A.logical_shift_right, A.bitwise_and))
-    v(V.tensor_scalar(T.s7[:], T.pi[:], 7, None, A.bitwise_and))
-    v(V.tensor_scalar(T.mj[:], T.mi[:], 7, None, A.bitwise_and))
-    v(V.tensor_scalar(T.rs[:], T.rs0[:], 0.5, None, A.is_gt))
-    vw()
 
+    wait(V, "z")
     wait(V, "du")
     for t in range(4):
         v(V.tensor_scalar(T.ut[:, t:512:4], T.zt[:, 0:128], T.us[:, t:t + 1], None, A.add))
@@ -114,9 +127,17 @@ def rank_program(g, core, T, topo):
     wait(P, "eq")
     inc(P.matmul_mx(T.sc[:, 0:128], T.qu[:], T.su[:], T.qx[:], T.sx[:], True, True), "pm")
 
+    wait(V, "gi")
+    v(V.tensor_scalar(T.ci[:, 0:1], T.pi[:], 248, None, A.bitwise_and))
+    v(V.tensor_scalar(T.ci[:, 1:2], T.pi[:], 64, None, A.bitwise_and))
+    v(V.tensor_scalar(T.ci[:, 2:3], T.pi[:], 56, None, A.bitwise_and))
+    v(V.tensor_scalar(T.mj[:], T.mi[:], 7, None, A.bitwise_and))
+    v(V.tensor_scalar(T.rs[:], T.rs0[:], 0.5, None, A.is_gt))
+
     wait(g, "eq")
     part = {d: [e for i, e in enumerate(engs(d)) if i // (len(engs(d)) // len(near)) == near.index(d)] for d in near}
-    for plane in (0, 1):
+
+    def send_halo(plane):
         tr = []
         for d in near:
             a, b = (120, 8) if d > r else (0, 144)
@@ -127,109 +148,133 @@ def rank_program(g, core, T, topo):
             tr.append(RemoteDMATransfer(dst_ids=[to(d)], dma_engine_mask=mask(part[d]), remote_sem=T.sem.halo,
                                         src=src, dst=dst))
         g.remote_dma_fused(tr, local_sem=T.sem.loc)
+
+    send_halo(0)
     halo = 0
     for d in near:
         nd = len([x for x in (d - 1, d + 1) if 0 <= x < N])
-        halo += 2 * (len(topo.engines(T.cores[d], core)) // nd)
+        halo += 2 * (len(engs(r, d)) // nd)
 
     wait(V, "pm")
-    inc(V.tensor_scalar(T.sg[:], T.sc[:, 0:128], -0.5, 0.5, A.max, A.min), "esg")
+    inc(V.tensor_scalar(T.sgp[:, 1:17, 1:9], T.sc[:, 0:128], -0.5, 0.5, A.max, A.min), "esg")
+    n1 = 120 if 0 < r < N - 1 else 128
+    b0 = ST * (n1 - 1)
     wait(S, "esg")
-    inc(S.activation(T.mg[:, r, 0:8], T.sg[:, 0:8], F.Copy), "s1")
-    inc(S.activation(T.mg[:, r, 26:34], T.sg[:, 120:128], F.Copy), "s1")
+    if r > 0:
+        inc(S.activation(T.mo[:, b0:b0 + 8], T.sgp[:, 1, 1:9], F.Copy, scale=4.0), "s1")
+    if r < N - 1:
+        inc(S.activation(T.mo[:, b0 + 25:b0 + 33], T.sgp[:, 16, 1:9], F.Copy, scale=4.0), "s1")
+    wait(S, "z")
+    wait(S, "dl")
+    for t in range(4):
+        inc(S.activation(T.ln[:, t:512:32], T.zt[:, 0:16], F.Copy), "sz")
+        inc(S.activation(T.rn[:, 28 + t:512:32], T.zt[:, 0:16], F.Copy), "sz")
     wait(V, "esg")
-    v(V.tensor_tensor(T.pq[:, 0:505:4], T.sg[:, 0:127], T.sc[:, 1:128], A.mult))
-    v(V.tensor_tensor(T.pq[:, 5:510:4], T.sg[:, 1:128], T.sc[:, 0:127], A.mult))
-    v(V.tensor_tensor(T.pq[:, 2:479:4], T.sg[:, 0:120], T.sc[:, 8:128], A.mult))
-    v(V.tensor_tensor(T.pq[:, 35:512:4], T.sg[:, 8:128], T.sc[:, 0:120], A.mult))
-    vw()
-    v(V.memset(T.pq[:, 28:512:32], 1.0))
-    v(V.memset(T.pq[:, 1:512:32], 1.0))
+    v(V.tensor_tensor(T.pq[:, 0:512:4], T.sgp[:, 1:17, 2:10], T.sc[:, 0:128], A.mult))
+    v(V.tensor_tensor(T.pq[:, 1:512:4], T.sgp[:, 1:17, 0:8], T.sc[:, 0:128], A.mult))
+    v(V.tensor_tensor(T.pq[:, 2:512:4], T.sgp[:, 2:18, 1:9], T.sc[:, 0:128], A.mult))
+    v(V.tensor_tensor(T.pq[:, 3:512:4], T.sgp[:, 0:16, 1:9], T.sc[:, 0:128], A.mult))
     vw()
     inc(V.tensor_tensor_scan(T.a4[:], T.ctl[:], T.pq[:], 0.0, A.max, A.min), "ea")
-
-    l1 = 120 if r < N - 1 else 128
-    l2 = 8 if r > 0 else 0
-    bias = (256 - (l1 + 128 - l2) / 2) / 2
-    wait(S, "ea")
-    inc(S.activation(T.j1[:, 0:l1], T.a4[:, 3:4 * l1:4], F.Sign, scale=-1.0, accum_out=T.acc[:, 0:1]), "s2")
-    inc(S.activation(T.j2[:, 0:128 - l2], T.a4[:, 3 + 4 * l2:512:4], F.Sign, scale=-1.0,
-                     accum_out=T.acc[:, 1:2]), "s2")
-    wait(S, "s2")
-    inc(S.activation(T.mg[:, r, 16:18], T.acc[:], F.Identity, bias=float(bias), scale=0.5), "s1")
     wait(V, "ea")
-    v(V.tensor_scalar(T.nn[:], T.a4[:, 3:512:4], 0.0, -4.0, A.is_gt, A.mult))
+    v(V.tensor_scalar(T.nnp[:, 8:136], T.a4[:, 3:512:4], 0.0, -4.0, A.is_ge, A.mult))
+    wait(V, "s1")
     vw()
-    inc(V.tensor_tensor(T.mg[:, r, 8:16], T.nn[:, 0:8], T.sg[:, 0:8], A.mult), "em")
-    inc(V.tensor_tensor(T.mg[:, r, 18:26], T.nn[:, 120:128], T.sg[:, 120:128], A.mult), "em")
-    m0, m1 = (16 if r == 0 else 0), (18 if r == N - 1 else 34)
+    d0, d1 = (8, 0) if r == 0 else (8, 16) if r == N - 1 else (8, 16)
+    inc(V.tensor_tensor_scan(T.mo[:, 16:b0 + 17:ST], T.nnp[:, d0:d0 + n1], T.nnp[:, d1:d1 + n1], 1024.0,
+                             A.add, A.add), "em")
+    if r > 0:
+        inc(V.tensor_tensor(T.mo[:, b0 + 8:b0 + 16], T.nnp[:, 8:16], T.sgp[:, 1, 1:9], A.mult), "em")
+    if r < N - 1:
+        inc(V.tensor_tensor(T.mo[:, b0 + 17:b0 + 25], T.nnp[:, 128:136], T.sgp[:, 16, 1:9], A.mult), "em")
+    m0, m1 = (16 if r == 0 else 0), (17 if r == N - 1 else 33)
     wait(g, "em")
     wait(g, "s1")
     g.remote_dma_fused([RemoteDMATransfer(dst_ids=[to(d) for d in others], dma_engine_mask=mask(engs(others[0])),
-                                          remote_sem=T.sem.msg, srcs=[T.mg[:, r, m0:m1]],
+                                          remote_sem=T.sem.msg, srcs=[T.mo[:, b0 + m0:b0 + m1]],
                                           dsts=[T.mg[:, r, m0:m1] for d in others])], local_sem=T.sem.loc)
-    g.sem_inc(T.sem.gm, 1)
-    Y.wait_ge(T.sem.gm, 1)
-    inc(Y.dma_start(T.wt[:, 2560:5120], T.w[:, 2560:5120]), "dw1", 16)
-    msg = sum(len(topo.engines(T.cores[d], core)) for d in others)
+    send_halo(1)
+    inc(g.iota(T.n0[:], [[1024, 4]], 64 * r, 0, allow_small_or_imprecise_dtypes=True), "gi3")
+    inc(g.iota(T.kr0[:], [[64, 5]], 0, 0, allow_small_or_imprecise_dtypes=True), "gi3")
+    msg = sum(len(engs(r, d)) for d in others)
+    wait(S, "em")
+    wait(S, "s1")
+    inc(S.activation(T.mg[:, r, m0:m1], T.mo[:, b0 + m0:b0 + m1], F.Copy), "so")
 
-    v(V.tensor_scalar(T.base[:, 8:120], T.nn[:, 8:120], 0.5, 2.0, A.mult, A.add))
-    v(V.tensor_scalar(T.base[:, 0:8], T.nn[:, 0:8], 0.25 if r > 0 else 0.5, 2.0, A.mult, A.add))
-    v(V.tensor_scalar(T.base[:, 120:128], T.nn[:, 120:128], 0.25 if r < N - 1 else 0.5, 2.0, A.mult, A.add))
-    for m in (0, 1):
-        v(V.tensor_scalar(T.c63[:, m:m + 1], T.e5[:], -2.0, 63.0 - 64.0 * m, A.mult, A.add))
-        v(V.tensor_scalar(T.c1[:, m:m + 1], T.e5[:], 2.0, 64.0 * m + 1.0, A.mult, A.add))
-    v(V.tensor_scalar(T.mh[:], T.mj[:], 0.0, 0.5, A.is_equal, A.mult))
-    v(V.tensor_scalar(T.m1[:], T.mj[:], 0.0, None, A.is_equal))
-    v(V.tensor_scalar(T.kk[:, 0:1], T.hi[:], -8.0, 80.0, A.mult, A.add))
-    v(V.tensor_scalar(T.kk[:, 1:2], T.hi[:], 136.0, 88.0, A.mult, A.add))
-    v(V.tensor_scalar(T.kk[:, 2:3], T.hi[:], 0.0, 352.0, A.mult, A.add))
+    inc(V.tensor_copy(T.cf[:], T.ci[:]), "ec")
+    inc(V.tensor_scalar(T.m1[:], T.mj[:], 0.0, None, A.is_equal), "ec")
+    wait(S, "ec")
+    wait(S, "gi2")
+    inc(S.activation(T.c1[:], T.i2[:], F.Identity, bias=T.cf[:, 0:1]), "sk")
+    inc(S.activation(T.kk[:, 0:1], T.cf[:, 1:2], F.Copy, bias=80.0, scale=-0.125), "sk")
+    inc(S.activation(T.kk[:, 1:2], T.cf[:, 1:2], F.Copy, bias=88.0, scale=2.125), "sk")
+    inc(S.activation(T.hs[:], T.cf[:, 1:2], F.Identity, bias=T.cf[:, 2:3], scale=8.0), "sk")
+    inc(S.activation(T.mh[:], T.m1[:], F.Copy, scale=0.5), "sk")
+    wait(S, "sk")
+    inc(S.activation(T.c63[:], T.c1[:], F.Copy, bias=256.0, scale=-1.0), "sk2")
+    v(V.tensor_scalar(T.base[:, 8:120], T.nnp[:, 16:128], 2.0, 8.0, A.mult, A.add))
+    v(V.tensor_scalar(T.base[:, 0:8], T.nnp[:, 8:16], 1.0 if r > 0 else 2.0, 8.0, A.mult, A.add))
+    v(V.tensor_scalar(T.base[:, 120:128], T.nnp[:, 128:136], 1.0 if r < N - 1 else 2.0, 8.0, A.mult, A.add))
+    v(V.memset(T.po[:], 0.0))
+    v(V.memset(T.pr[:, 112:120], 0.0))
+    v(V.memset(T.zt[:, 128:512], 0.0))
+    vw()
     if r == 0:
         v(V.quantize_mx(T.wx[:, 8:136], T.swx[:, 8:136], T.zt[:]))
+        vw()
     if r == N - 1:
         v(V.quantize_mx(T.wx[:, 24:152], T.swx[:, 24:152], T.zt[:]))
-    wait(V, "dl")
-    for t in range(4):
-        v(V.memset(T.ln[:, t:512:32], 0.0))
-        v(V.memset(T.rn[:, 28 + t:512:32], 0.0))
-    vw()
+        vw()
     v(V.quantize_mx(T.wx[:, 16:144], T.swx[:, 16:144], T.xs[:]))
+    wait(V, "sz")
     v(V.quantize_mx(T.wx[:, 160:288], T.swx[:, 160:288], T.ln[:]))
     v(V.quantize_mx(T.wx[:, 288:416], T.swx[:, 288:416], T.rn[:]))
+    wait(V, "dw0")
+    inc(V.quantize_mx(T.qw[:, 0:384], T.sw[:, 0:384], T.wt[:, 0:1536]), "ew")
     vw()
 
-    V.wait_ge(T.sem.msg, msg)
-    wait(V, "s1")
-    wait(V, "em")
     if r > 0:
-        v(V.tensor_tensor(T.po[:, 0:8], T.mg[:, r, 8:16], T.mg[:, r - 1, 26:34], A.mult))
+        S.wait_ge(T.sem.msg, msg)
+        inc(S.activation(T.jr[:, 0:r], T.mg[:, 0:r, 16], F.Copy, accum_out=T.cr[:]), "ecr")
+    V.wait_ge(T.sem.msg, msg)
+    wait(V, "so")
+    inc(V.tensor_tensor(T.pr[:, 0:112], T.mg[:, 0:N - 1, 17:33], T.mg[:, 1:N, 0:16], A.mult), "v")
+    if r > 0:
+        v(V.tensor_tensor(T.po[:, 0:8], T.mg[:, r, 8:16], T.mg[:, r - 1, 25:33], A.mult))
     if r < N - 1:
-        v(V.tensor_tensor(T.po[:, 120:128], T.mg[:, r, 18:26], T.mg[:, r + 1, 0:8], A.mult))
-    v(V.tensor_tensor_scan(T.cc[:], T.mg[:, :, 16], T.mg[:, :, 17], 0.0, A.add, A.add))
-    v(V.tensor_tensor(T.pr[:], T.mg[:, 0:N - 1, 18:34], T.mg[:, 1:N, 0:16], A.mult))
+        v(V.tensor_tensor(T.po[:, 120:128], T.mg[:, r, 17:25], T.mg[:, r + 1, 0:8], A.mult))
     vw()
-    v(V.tensor_tensor_scan(T.cs[:], T.zt[:, 0:112], T.pr[:], T.cc[:, r - 1:r] if r > 0 else 0.0, A.add, A.add))
-    v(V.tensor_tensor_scan(T.rr[:], T.base[:], T.po[:], 0.0, A.add, A.add))
+    if r > 0:
+        wait(V, "ecr")
+    v(V.tensor_tensor_scan(T.cs[:], T.zt[:, 0:120], T.pr[:], T.cr[:] if r > 0 else 0.0, A.add, A.add))
+    inc(V.tensor_tensor_scan(T.rr[:], T.base[:], T.po[:], 0.0, A.add, A.add), "err")
+    wait(V, "sk")
+    wait(V, "sk2")
     vw()
-    if r == 0:
-        inc(V.tensor_copy(T.thr[:], T.c1[:]), "eth")
-    else:
-        a2 = T.cs[:, 16 * r - 9:16 * r - 8]
-        v(V.tensor_scalar(T.tb[:], T.c63[:], a2, BIG, A.add, A.add))
-        v(V.tensor_scalar(T.tw[:], T.c1[:], a2, None, A.subtract))
+    thr = T.c1
+    if r > 0:
+        thr = T.thr
+        a8 = T.cs[:, 16 * r - 9:16 * r - 8]
+        v(V.tensor_scalar(T.tb[:], T.c63[:], a8, BIG, A.add, A.add))
+        v(V.tensor_scalar(T.tw[:], T.c1[:], a8, None, A.subtract))
         vw()
         inc(V.tensor_scalar(T.thr[:, 0:1], T.tb[:, 0:1], BIG, T.tw[:, 0:1], A.subtract, A.add), "eth")
         v(V.tensor_scalar(T.thr[:, 1:2], T.tb[:, 1:2], BIG, T.tw[:, 1:2], A.subtract, A.add))
-    wait(S, "eth")
-    inc(S.activation(T.j3[:], T.rr[:], F.Sign, bias=T.thr[:, 0:1], scale=-1.0, accum_out=T.acl[:]), "sa")
+        wait(S, "eth")
+    wait(S, "err")
+    wait(S, "sk2")
+    inc(S.activation(T.j3[:], T.rr[:], F.Sign, bias=thr[:, 0:1], scale=-1.0, accum_out=T.acl[:]), "sa")
     wait(S, "sa")
     inc(S.activation(T.it[:, 0:32], T.mh[:], F.Copy, scale=T.acl[:]), "et")
     vw()
-    wait(V, "eth")
-    v(V.tensor_scalar(T.cm[:], T.rr[:], T.thr[:, 1:2], 0.5, A.is_le, A.subtract))
+    wait(V, "err")
+    if r > 0:
+        wait(V, "eth")
+    v(V.tensor_scalar(T.cm[:], T.rr[:], thr[:, 1:2], 0.5, A.is_le, A.subtract))
     vw()
     v(V.tensor_reduce(T.cl1[:], T.cm[:], AxisListType.X, A.add))
     vw()
+    wait(V, "ec")
     v(V.tensor_scalar(T.it[:, 32:64], T.m1[:], T.cl1[:], None, A.mult))
     vw()
     wait(V, "et")
@@ -237,52 +282,55 @@ def rank_program(g, core, T, topo):
     vw()
     v(V.tensor_tensor_scan(T.ss[:], T.rs[:], T.tt[:], 0.0, A.mult, A.add))
     vw()
-    for k in range(3):
-        inc(V.tensor_scalar(T.off[:, k:24:3], T.ss[:, 7:64:8], 63.0, T.kk[:, k:k + 1], A.min, A.add), "eo")
-    wait(V, "eo")
-    V.wait_ge(T.sem.halo, halo)
-    inc(V.tensor_copy(T.slot[:].bitcast(dt.uint32), T.wx[:].bitcast(dt.uint32).indirect(T.off[:])), "ep")
-    wait(S, "eo")
-    S.wait_ge(T.sem.halo, halo)
-    inc(S.activation(T.sslot[:], T.swx[:].indirect(T.off[:]), F.Copy), "es")
+    kk = [T.kk[:, 0:1], T.kk[:, 1:2], 352.0]
+    for b in (0, 1):
+        h = "ab"[b]
+        off, par = T["off" + h], (r + 1 + b) % 2
+        for k in range(3):
+            inc(V.tensor_scalar(off[:, k:12:3], T.ss[:, 7 + 8 * par:64:16], 63.0, kk[k], A.min, A.add), "eo" + h)
+        for q in (V, S):
+            wait(q, "eo" + h)
+            if b == 0:
+                q.wait_ge(T.sem.halo, halo)
+        inc(V.tensor_copy(T["slot" + h][:].bitcast(dt.uint32), T.wx[:].bitcast(dt.uint32).indirect(off[:])), "ep" + h)
+        inc(S.activation(T["sslot" + h][:], T.swx[:].indirect(off[:]), F.Copy), "es" + h)
+        for plane in (0, 1):
+            wait(g, ("es" if plane else "ep") + h)
+            tr = []
+            for d, es in deal(r, b, plane).items():
+                i = 48 * (d // 2)
+                if plane:
+                    src, dst = T["sslot" + h][:, i:i + 40], T.sland[:, 48 * r:48 * r + 40]
+                else:
+                    src = T["slot" + h][:, i:i + 40].bitcast(dt.uint8)
+                    dst = T.land[:, 48 * r:48 * r + 40].bitcast(dt.uint8)
+                tr.append(RemoteDMATransfer(dst_ids=[to(d)], dma_engine_mask=mask(es), remote_sem=T.sem.cod,
+                                            src=src, dst=dst))
+            g.remote_dma_fused(tr, local_sem=T.sem.loc)
+    cod = 0
+    for s in others:
+        for b in (0, 1):
+            for plane in (0, 1):
+                cod += len(deal(s, b, plane).get(r, []))
 
-    for plane in (0, 1):
-        wait(g, "es" if plane else "ep")
-        tr = []
-        for i, d in enumerate(others):
-            if plane:
-                src, dst = T.sslot[:, 48 * d:48 * d + 40], T.sland[:, 48 * r:48 * r + 40]
-            else:
-                src = T.slot[:, 48 * d:48 * d + 40].bitcast(dt.uint8)
-                dst = T.land[:, 48 * r:48 * r + 40].bitcast(dt.uint8)
-            tr.append(RemoteDMATransfer(dst_ids=[to(d)], dma_engine_mask=mask([engs(d)[i]]), remote_sem=T.sem.cod,
-                                        src=src, dst=dst))
-        g.remote_dma_fused(tr, local_sem=T.sem.loc)
-
     for k in range(3):
-        inc(V.tensor_scalar(T.offo[:, k:k + 1], T.ss[:, 8 * r + 7:8 * r + 8], 63.0, T.kk[:, k:k + 1],
-                            A.min, A.add), "eo2")
+        inc(V.tensor_scalar(T.offo[:, k:k + 1], T.ss[:, 8 * r + 7:8 * r + 8], 63.0, kk[k], A.min, A.add), "eo2")
+    v(V.tensor_tensor_scan(T.cc[:], T.mg[:, :, 16], T.zt[:, 0:8], 0.0, A.add, A.add))
+    wait(V, "gi3")
+    v(V.tensor_scalar(T.kr[:], T.kr0[:], T.cf[:, 2:3], 0.125, A.add, A.mult))
+    if r > 0:
+        v(V.tensor_scalar(T.n2[:], T.n0[:], T.hs[:], T.cr[:], A.add, A.add))
+    else:
+        v(V.tensor_scalar(T.n2[:], T.n0[:], T.hs[:], None, A.add))
     wait(V, "eo2")
     inc(V.tensor_copy(T.land[:, 48 * r:48 * r + 48].bitcast(dt.uint32),
                       T.wx[:].bitcast(dt.uint32).indirect(T.offo[:, 0:3])), "ep2")
     wait(S, "eo2")
     inc(S.activation(T.sland[:, 48 * r:48 * r + 48], T.swx[:].indirect(T.offo[:, 0:3]), F.Copy), "es2")
-
+    vw()
+    v(V.tensor_tensor(T.aq[:], T.cc[:], T.cs[:, 7:120:16], A.add))
     v(V.quantize_mx(T.land[:, 384:512], T.sland[:, 384:512], T.zt[:]))
     v(V.quantize_mx(T.mv[:, 320:448], T.smv[:, 320:448], T.zt[:]))
-
-    v(V.tensor_scalar(T.hs[:, 0:1], T.s7[:], 1.0, None, A.mult))
-    v(V.tensor_scalar(T.hs[:, 1:2], T.hi[:], 128.0, None, A.mult))
-    v(V.tensor_tensor(T.aq[:, 0:7], T.cc[:, 0:7], T.cs[:, 7:112:16], A.add))
-    v(V.tensor_tensor(T.aq[:, 7:8], T.cc[:, 7:8], T.cs[:, 111:112], A.add))
-    vw()
-    v(V.tensor_scalar(T.kr[:], T.kr0[:], T.hs[:, 0:1], None, A.add))
-    v(V.tensor_scalar(T.n2[:], T.n0[:], T.hs[:, 0:1], T.hs[:, 1:2], A.add, A.add))
-    vw()
-    if r > 0:
-        v(V.tensor_scalar(T.n2[:], T.n2[:], T.hs[:, 0:1], T.cc[:, r - 1:r], A.add, A.add))
-    else:
-        v(V.tensor_scalar(T.n2[:], T.n2[:], T.hs[:, 0:1], None, A.add))
     vw()
     for c in range(4):
         v(V.tensor_scalar(T.cq[:, 8 * c:8 * c + 8], T.aq[:], T.n2[:, c:c + 1], 48.0, A.is_le, A.mult))
@@ -292,31 +340,30 @@ def rank_program(g, core, T, topo):
     for k in range(5):
         inc(V.tensor_scalar(T.offr[:, 4 * k:4 * k + 4], T.sq[:, 7:32:8], T.kr[:, k:k + 1], None, A.add), "er")
 
-    wait(V, "dw0")
-    inc(V.quantize_mx(T.qw[:, 0:512], T.sw[:, 0:512], T.wt[:, 0:2048]), "ew")
     wait(V, "dw1")
-    inc(V.quantize_mx(T.qw[:, 512:1024], T.sw[:, 512:1024], T.wt[:, 2048:4096]), "ew")
-    inc(V.quantize_mx(T.qw[:, 1024:1280], T.sw[:, 1024:1280], T.wt[:, 4096:5120]), "ew")
+    inc(V.quantize_mx(T.qw[:, 384:896], T.sw[:, 384:896], T.wt[:, 1536:3584]), "ew")
+    inc(V.quantize_mx(T.qw[:, 896:1280], T.sw[:, 896:1280], T.wt[:, 3584:5120]), "ew")
+    vw()
 
     for q in (V, S):
         wait(q, "er")
         wait(q, "ep2")
         wait(q, "es2")
-        q.wait_ge(T.sem.cod, 2 * len(others))
+        q.wait_ge(T.sem.cod, cod)
     wait(P, "ew")
     for k in range(5):
-        o16 = T.offr[:, 4 * k:4 * k + 4]
-        inc(V.tensor_copy(T.mv[:, 64 * k:64 * k + 64].bitcast(dt.uint32),
+        o16, at = T.offr[:, 4 * k:4 * k + 4], 64 * (4 - k)
+        inc(V.tensor_copy(T.mv[:, at:at + 64].bitcast(dt.uint32),
                           T.land[:].bitcast(dt.uint32).indirect(o16)), "kv%d" % k)
-        inc(S.activation(T.smv[:, 64 * k:64 * k + 64], T.sland[:].indirect(o16), F.Copy), "ks%d" % k)
+        inc(S.activation(T.smv[:, at:at + 64], T.sland[:].indirect(o16), F.Copy), "ks%d" % k)
     for k in range(5):
-        for kk in ([0, 1] if k == 0 else [k + 1] if k < 4 else []):
-            wait(P, "kv%d" % kk)
-            wait(P, "ks%d" % kk)
+        at = 64 * (4 - k)
+        wait(P, "kv%d" % k)
+        wait(P, "ks%d" % k)
         for o in (0, 1):
             w0 = 128 * (2 * k + o)
             i = P.matmul_mx(T.ps[:, 512 * o:512 * o + 128], T.qw[:, w0:w0 + 128], T.sw[:, w0:w0 + 128],
-                            T.mv[:, 64 * k:64 * k + 128], T.smv[:, 64 * k:64 * k + 128], k == 0, k == 4)
+                            T.mv[:, at:at + 128], T.smv[:, at:at + 128], k == 0, k == 4)
             if k == 4:
                 inc(i, "py%d" % o)
     wait(V, "py0")
@@ -328,5 +375,4 @@ def rank_program(g, core, T, topo):
     wait(S, "ys")
     inc(S.dma_start(T.y[:, 64:128], T.yo[:, 64:128]), "dy", 16)
     wait(Y, "dy")
-    vw()
-    g.wait_ge(T.sem.loc, 3 * len(engs(others[0])) + 2 * len(others))
+    g.wait_ge(T.sem.loc, 7 * len(engs(others[0])))

@@ -5,9 +5,11 @@ A = AluOpType
 F = ActivationFunctionType
 C4, U8 = "float8_e4m3fn_x4", "uint8"
 BF, F32 = "bfloat16", "float32"
-HUGE = 1e29
 BIG = 1.5 * 2.0 ** 32
 ST = 40
+W0 = 2560
+BATCH = ((0, 1, 2), (4, 5, 6, 7))
+OWN = 3
 SCRATCH = {
     "xs": ("sbuf", [128, 512], BF), "us": ("sbuf", [128, 4], BF), "ut": ("sbuf", [128, 512], BF),
     "ln": ("sbuf", [128, 512], BF), "rn": ("sbuf", [128, 512], BF), "zt": ("sbuf", [128, 512], BF),
@@ -15,38 +17,39 @@ SCRATCH = {
     "qu": ("sbuf", [128, 128], C4), "su": ("sbuf", [128, 128], U8),
     "qx": ("sbuf", [128, 128], C4), "sx": ("sbuf", [128, 128], U8),
     "wx": ("sbuf", [128, 416], C4), "swx": ("sbuf", [128, 416], U8),
-    "slota": ("sbuf", [128, 192], C4), "sslota": ("sbuf", [128, 192], U8),
+    "slota": ("sbuf", [128, 144], C4), "sslota": ("sbuf", [128, 144], U8),
     "slotb": ("sbuf", [128, 192], C4), "sslotb": ("sbuf", [128, 192], U8),
     "land": ("sbuf", [128, 512], C4), "sland": ("sbuf", [128, 512], U8),
     "mv": ("sbuf", [128, 448], C4), "smv": ("sbuf", [128, 448], U8),
     "qw": ("sbuf", [128, 1280], C4), "sw": ("sbuf", [128, 1280], U8),
-    "sgp": ("sbuf", [128, 18, 10], BF), "pq": ("sbuf", [128, 512], BF), "ctl": ("sbuf", [128, 512], BF),
-    "a4": ("sbuf", [128, 512], BF), "nnp": ("sbuf", [128, 144], BF),
+    "sgp": ("sbuf", [128, 18, 10], BF), "nb": ("sbuf", [128, 640], BF), "ow": ("sbuf", [128, 640], BF),
+    "a4": ("sbuf", [128, 640], BF), "nnp": ("sbuf", [128, 144], BF),
     "mo": ("sbuf", [128, ST * 128], BF), "mg": ("sbuf", [128, 8, 40], BF), "jr": ("sbuf", [128, 8], F32),
-    "cr": ("sbuf", [128, 1], F32), "j3": ("sbuf", [128, 128], F32),
-    "base": ("sbuf", [128, 128], BF), "po": ("sbuf", [128, 128], BF), "pr": ("sbuf", [128, 120], BF),
-    "cc": ("sbuf", [128, 8], F32), "cs": ("sbuf", [128, 120], F32), "aq": ("sbuf", [128, 8], F32),
+    "cr": ("sbuf", [128, 1], F32), "cr2": ("sbuf", [128, 1], F32), "j3": ("sbuf", [128, 128], F32),
+    "base": ("sbuf", [128, 128], BF), "po": ("sbuf", [128, 128], BF),
+    "pa": ("sbuf", [128, 64], BF), "za": ("sbuf", [128, 64], BF), "cA": ("sbuf", [128, 64], F32),
+    "cB": ("sbuf", [128, 64], F32), "pf": ("sbuf", [128, 64], BF), "zf": ("sbuf", [128, 64], BF),
+    "cc": ("sbuf", [128, 8], F32), "cs": ("sbuf", [128, 64], F32), "aq": ("sbuf", [128, 8], F32),
     "rr": ("sbuf", [128, 128], BF),
     "pi": ("sbuf", [128, 1], "int32"), "ci": ("sbuf", [128, 3], "int32"), "cf": ("sbuf", [128, 3], F32),
-    "mi": ("sbuf", [128, 32], "int32"), "mj": ("sbuf", [128, 32], "int32"), "i2": ("sbuf", [128, 2], F32),
+    "mi": ("sbuf", [128, 32], "int32"), "mj": ("sbuf", [128, 32], "int32"), "i2": ("sbuf", [128, 1], F32),
     "rs0": ("sbuf", [128, 64], F32), "rs": ("sbuf", [128, 64], F32),
-    "c63": ("sbuf", [128, 2], F32), "c1": ("sbuf", [128, 2], F32), "mh": ("sbuf", [128, 32], F32),
+    "c1": ("sbuf", [128, 1], F32), "mh": ("sbuf", [128, 32], F32),
     "m1": ("sbuf", [128, 32], F32), "kk": ("sbuf", [128, 2], F32), "hs": ("sbuf", [128, 1], F32),
-    "tb": ("sbuf", [128, 2], F32), "tw": ("sbuf", [128, 2], F32), "thr": ("sbuf", [128, 2], F32),
-    "cm": ("sbuf", [128, 128], BF), "acl": ("sbuf", [128, 1], F32), "cl1": ("sbuf", [128, 1], F32),
+    "thr": ("sbuf", [128, 1], F32),
+    "cm": ("sbuf", [128, 128], BF), "acl": ("sbuf", [128, 1], F32), "cn": ("sbuf", [128, 128], BF),
     "it": ("sbuf", [128, 64], F32), "tt": ("sbuf", [128, 64], F32), "ss": ("sbuf", [128, 64], F32),
-    "offa": ("sbuf", [128, 12], "uint16"), "offb": ("sbuf", [128, 12], "uint16"),
-    "offo": ("sbuf", [128, 4], "uint16"),
+    "off": ("sbuf", [128, 24], "uint16"), "offo": ("sbuf", [128, 4], "uint16"),
     "n0": ("sbuf", [128, 4], F32), "n2": ("sbuf", [128, 4], F32),
     "kr0": ("sbuf", [128, 5], F32), "kr": ("sbuf", [128, 5], F32), "cq": ("sbuf", [128, 32], F32),
     "sq": ("sbuf", [128, 32], F32), "offr": ("sbuf", [128, 20], "uint16"),
     "yo": ("sbuf", [128, 128], F32),
     "sc": ("psum", [128, 512], F32), "ps": ("psum", [128, 1024], F32),
 }
-SEMAPHORES = ["v", "z", "du", "dx", "dl", "dw0", "dw1", "gi", "gi2", "gi3", "eu", "eq", "pm", "esg", "s1", "ea", "em",
-              "so", "sz", "ec", "sk", "sk2", "ecr", "eth", "err", "sa", "et", "eoa", "epa", "esa", "eob", "epb", "esb",
-              "eo2", "ep2", "es2", "ew", "er", "py0", "py1", "yv", "ys", "dy",
-              "halo", "msg", "cod", "loc"] + ["kv%d" % k for k in range(5)] + ["ks%d" % k for k in range(5)]
+SEMAPHORES = ["v", "z", "du", "dx", "dl", "dw0", "dw1", "gi", "gi2", "gi3", "ect", "eut", "eu", "eq", "pm", "esg", "eow",
+              "s1", "ea", "em", "so", "sz", "ec", "eza", "sk", "sk2", "ecr", "ecr2", "eth", "err", "sa", "et", "eo", "epa",
+              "esa", "epb", "esb", "eo2", "ep2", "es2", "ew", "er", "py0", "py1", "yv", "ys", "dy", "vp", "vq", "va", "vb",
+              "halo", "msg", "cod", "loc", "lm"] + ["kv%d" % k for k in range(5)] + ["ks%d" % k for k in range(5)]
 
 
 def rank_program(g, core, T, topo):
@@ -80,14 +83,15 @@ def rank_program(g, core, T, topo):
     def mask(es):
         return int(sum(1 << e for e in es))
 
-    others = [d for d in range(N) if d != r]
-    near = [d for d in (r - 1, r + 1) if 0 <= d < N]
+    others = [(r + j) % N for j in range(1, N)]
 
-    def batch(s, b):
-        return [(s + j) % N for j in range(1, N) if j % 2 == 1 - b]
+    def nears(s):
+        return [d for d in (s - 1, s + 1) if 0 <= d < N]
+
+    near = nears(r)
 
     def deal(s, b, plane):
-        ds = batch(s, b)
+        ds = [(s + j - OWN) % N for j in BATCH[b]]
         es = engs(ds[0], s)
         n = len(es) // 4
         w = [1] * 4 if len(ds) == 4 else [2, 1, 1] if plane else [1, 1, 2]
@@ -101,24 +105,33 @@ def rank_program(g, core, T, topo):
     inc(Y.dma_start(T.xs[:], T.x[:]), "dx", 16)
     inc(S.dma_start(T.ln[:, 4:512], T.x[:, 0:508]), "dl", 16)
     inc(Y.dma_start(T.rn[:, 0:508], T.x[:, 4:512]), "dl", 16)
-    inc(Y.dma_start(T.wt[:, 0:2560], T.w[:, 0:2560]), "dw0", 16)
-    inc(Y.dma_start(T.wt[:, 2560:5120], T.w[:, 2560:5120]), "dw1", 16)
+    inc(Y.dma_start(T.wt[:, 0:W0], T.w[:, 0:W0]), "dw0", 16)
 
     inc(g.iota(T.pi[:], [[1, 1]], 0, 8), "gi")
     inc(g.iota(T.mi[:], [[1, 32]], 256, -1), "gi")
     inc(g.iota(T.rs0[:], [[0, 8], [1, 8]], 0, 0, allow_small_or_imprecise_dtypes=True), "gi")
-    inc(g.iota(T.i2[:], [[256, 2]], 4, 0, allow_small_or_imprecise_dtypes=True), "gi2")
-    inc(V.memset(T.zt[:, 0:128], 0.0), "z")
-    v(V.memset(T.ctl[:], -HUGE))
+    inc(g.iota(T.i2[:], [[0, 1]], 4, 0, allow_small_or_imprecise_dtypes=True), "gi2")
+    inc(V.memset(T.zt[:], 0.0), "z")
+    v(V.memset(T.ow[:], 1.0))
     v(V.memset(T.sgp[:], 0.0))
     v(V.memset(T.nnp[:], 0.0))
     vw()
-    v(V.memset(T.ctl[:, 0:512:4], HUGE))
+    v(V.memset(T.ow[:, 0:640:5], 0.0))
 
+    wait(S, "z")
+    inc(S.activation(T.nb[:, 4:640:5], T.zt[:, 0:128], F.Copy, bias=-1.0), "ect")
+    wait(S, "ect")
+    for a, b, st, k, c in ((9, 39, 5, 6, -0.75), (609, 639, 5, 6, -0.75), (44, 600, 40, 14, -0.75), (79, 600, 40, 14, -0.75),
+                           (4, 40, 35, 2, -0.5), (604, 640, 35, 2, -0.5)):
+        inc(S.activation(T.nb[:, a:b:st], T.zt[:, 0:k], F.Copy, bias=c), "ect")
+
+    wait(S, "du")
+    inc(S.activation(T.ut[:, 3:512:4], T.zt[:, 0:128], F.Identity, bias=T.us[:, 3:4]), "eut")
     wait(V, "z")
     wait(V, "du")
-    for t in range(4):
+    for t in range(3):
         v(V.tensor_scalar(T.ut[:, t:512:4], T.zt[:, 0:128], T.us[:, t:t + 1], None, A.add))
+    wait(V, "eut")
     vw()
     inc(V.quantize_mx(T.qu[:], T.su[:], T.ut[:]), "eu")
     wait(V, "dx")
@@ -127,60 +140,50 @@ def rank_program(g, core, T, topo):
     wait(P, "eq")
     inc(P.matmul_mx(T.sc[:, 0:128], T.qu[:], T.su[:], T.qx[:], T.sx[:], True, True), "pm")
 
-    wait(V, "gi")
-    v(V.tensor_scalar(T.ci[:, 0:1], T.pi[:], 248, None, A.bitwise_and))
-    v(V.tensor_scalar(T.ci[:, 1:2], T.pi[:], 64, None, A.bitwise_and))
-    v(V.tensor_scalar(T.ci[:, 2:3], T.pi[:], 56, None, A.bitwise_and))
-    v(V.tensor_scalar(T.mj[:], T.mi[:], 7, None, A.bitwise_and))
-    v(V.tensor_scalar(T.rs[:], T.rs0[:], 0.5, None, A.is_gt))
-
-    wait(g, "eq")
-    part = {d: [e for i, e in enumerate(engs(d)) if i // (len(engs(d)) // len(near)) == near.index(d)] for d in near}
-
-    def send_halo(plane):
+    def send_halo(plane, ds, sent):
         tr = []
-        for d in near:
+        for i, d in enumerate(ds):
             a, b = (120, 8) if d > r else (0, 144)
+            es = engs(d)
+            n = len(es) // len(ds)
             if plane:
                 src, dst = T.sx[:, a:a + 8], T.swx[:, b:b + 8]
             else:
                 src, dst = T.qx[:, a:a + 8].bitcast(dt.uint8), T.wx[:, b:b + 8].bitcast(dt.uint8)
-            tr.append(RemoteDMATransfer(dst_ids=[to(d)], dma_engine_mask=mask(part[d]), remote_sem=T.sem.halo,
+            tr.append(RemoteDMATransfer(dst_ids=[to(d)], dma_engine_mask=mask(es[n * i:n * i + n]), remote_sem=T.sem.halo,
                                         src=src, dst=dst))
-        g.remote_dma_fused(tr, local_sem=T.sem.loc)
+        g.remote_dma_fused(tr, local_sem=T.sem[sent])
 
-    send_halo(0)
-    halo = 0
-    for d in near:
-        nd = len([x for x in (d - 1, d + 1) if 0 <= x < N])
-        halo += 2 * (len(engs(r, d)) // nd)
+    wait(g, "eq")
+    send_halo(1, near[:1], "lm")
+    halo = sum(len(engs(r, d)) + len(engs(r, d)) // len(nears(d)) for d in near)
 
     wait(V, "pm")
     inc(V.tensor_scalar(T.sgp[:, 1:17, 1:9], T.sc[:, 0:128], -0.5, 0.5, A.max, A.min), "esg")
     n1 = 120 if 0 < r < N - 1 else 128
     b0 = ST * (n1 - 1)
     wait(S, "esg")
+    inc(S.activation(T.ow[:, 4:640:5], T.sgp[:, 1:17, 1:9], F.Copy), "eow")
     if r > 0:
         inc(S.activation(T.mo[:, b0:b0 + 8], T.sgp[:, 1, 1:9], F.Copy, scale=4.0), "s1")
     if r < N - 1:
         inc(S.activation(T.mo[:, b0 + 25:b0 + 33], T.sgp[:, 16, 1:9], F.Copy, scale=4.0), "s1")
-    wait(S, "z")
     wait(S, "dl")
     for t in range(4):
         inc(S.activation(T.ln[:, t:512:32], T.zt[:, 0:16], F.Copy), "sz")
         inc(S.activation(T.rn[:, 28 + t:512:32], T.zt[:, 0:16], F.Copy), "sz")
     wait(V, "esg")
-    v(V.tensor_tensor(T.pq[:, 0:512:4], T.sgp[:, 1:17, 2:10], T.sc[:, 0:128], A.mult))
-    v(V.tensor_tensor(T.pq[:, 1:512:4], T.sgp[:, 1:17, 0:8], T.sc[:, 0:128], A.mult))
-    v(V.tensor_tensor(T.pq[:, 2:512:4], T.sgp[:, 2:18, 1:9], T.sc[:, 0:128], A.mult))
-    v(V.tensor_tensor(T.pq[:, 3:512:4], T.sgp[:, 0:16, 1:9], T.sc[:, 0:128], A.mult))
+    for k, (a, b) in enumerate(((1, 2), (1, 0), (2, 1), (0, 1))):
+        v(V.tensor_scalar(T.nb[:, k:640:5], T.sgp[:, a:a + 16, b:b + 8], 1.0, None, A.mult))
+    wait(V, "ect")
+    wait(V, "eow")
     vw()
-    inc(V.tensor_tensor_scan(T.a4[:], T.ctl[:], T.pq[:], 0.0, A.max, A.min), "ea")
+    inc(V.tensor_tensor_scan(T.a4[:], T.ow[:], T.nb[:], 0.0, A.mult, A.add), "ea")
     wait(V, "ea")
-    v(V.tensor_scalar(T.nnp[:, 8:136], T.a4[:, 3:512:4], 0.0, -4.0, A.is_ge, A.mult))
+    v(V.tensor_scalar(T.nnp[:, 8:136], T.a4[:, 4:640:5], 0.0, -4.0, A.is_ge, A.mult))
     wait(V, "s1")
     vw()
-    d0, d1 = (8, 0) if r == 0 else (8, 16) if r == N - 1 else (8, 16)
+    d0, d1 = (8, 0) if r == 0 else (8, 16)
     inc(V.tensor_tensor_scan(T.mo[:, 16:b0 + 17:ST], T.nnp[:, d0:d0 + n1], T.nnp[:, d1:d1 + n1], 1024.0,
                              A.add, A.add), "em")
     if r > 0:
@@ -192,8 +195,12 @@ def rank_program(g, core, T, topo):
     wait(g, "s1")
     g.remote_dma_fused([RemoteDMATransfer(dst_ids=[to(d) for d in others], dma_engine_mask=mask(engs(others[0])),
                                           remote_sem=T.sem.msg, srcs=[T.mo[:, b0 + m0:b0 + m1]],
-                                          dsts=[T.mg[:, r, m0:m1] for d in others])], local_sem=T.sem.loc)
-    send_halo(1)
+                                          dsts=[T.mg[:, r, m0:m1] for d in others])], local_sem=T.sem.lm)
+    send_halo(0, near, "loc")
+    Y.wait_ge(T.sem.lm, 2 * len(engs(others[0])))
+    inc(Y.dma_start(T.wt[:, W0:5120], T.w[:, W0:5120]), "dw1", 16)
+    if near[1:]:
+        send_halo(1, near[1:], "loc")
     inc(g.iota(T.n0[:], [[1024, 4]], 64 * r, 0, allow_small_or_imprecise_dtypes=True), "gi3")
     inc(g.iota(T.kr0[:], [[64, 5]], 0, 0, allow_small_or_imprecise_dtypes=True), "gi3")
     msg = sum(len(engs(r, d)) for d in others)
@@ -201,6 +208,18 @@ def rank_program(g, core, T, topo):
     wait(S, "s1")
     inc(S.activation(T.mg[:, r, m0:m1], T.mo[:, b0 + m0:b0 + m1], F.Copy), "so")
 
+    E = 8 * r
+    wait(V, "gi")
+    v(V.tensor_scalar(T.ci[:, 0:1], T.pi[:], 248, None, A.bitwise_and))
+    v(V.tensor_scalar(T.ci[:, 1:2], T.pi[:], 64, None, A.bitwise_and))
+    v(V.tensor_scalar(T.ci[:, 2:3], T.pi[:], 56, None, A.bitwise_and))
+    v(V.tensor_scalar(T.mj[:], T.mi[:], 7, None, A.bitwise_and))
+    v(V.tensor_scalar(T.rs[:], T.rs0[:], 0.5, None, A.is_gt))
+    if r > 0:
+        inc(V.memset(T.za[:, 0:E], 0.0), "eza")
+    inc(V.memset(T.za[:, E + 1:E + 2], -BIG), "eza")
+    inc(V.memset(T.pa[:, E:E + 1], BIG), "eza")
+    vw()
     inc(V.tensor_copy(T.cf[:], T.ci[:]), "ec")
     inc(V.tensor_scalar(T.m1[:], T.mj[:], 0.0, None, A.is_equal), "ec")
     wait(S, "ec")
@@ -211,14 +230,15 @@ def rank_program(g, core, T, topo):
     inc(S.activation(T.hs[:], T.cf[:, 1:2], F.Identity, bias=T.cf[:, 2:3], scale=8.0), "sk")
     inc(S.activation(T.mh[:], T.m1[:], F.Copy, scale=0.5), "sk")
     wait(S, "sk")
-    inc(S.activation(T.c63[:], T.c1[:], F.Copy, bias=256.0, scale=-1.0), "sk2")
+    sh = 64 * ((r - OWN) % N)
+    inc(S.activation(T.za[:, E:E + 1], T.c1[:], F.Copy, bias=256.0 - sh, scale=-1.0), "sk2")
+    inc(S.activation(T.pa[:, E + 1:E + 2], T.c1[:], F.Copy, bias=float(sh)), "sk2")
     v(V.tensor_scalar(T.base[:, 8:120], T.nnp[:, 16:128], 2.0, 8.0, A.mult, A.add))
     v(V.tensor_scalar(T.base[:, 0:8], T.nnp[:, 8:16], 1.0 if r > 0 else 2.0, 8.0, A.mult, A.add))
     v(V.tensor_scalar(T.base[:, 120:128], T.nnp[:, 128:136], 1.0 if r < N - 1 else 2.0, 8.0, A.mult, A.add))
     v(V.memset(T.po[:], 0.0))
-    v(V.memset(T.pr[:, 112:120], 0.0))
-    v(V.memset(T.zt[:, 128:512], 0.0))
-    vw()
+    v(V.memset(T.pf[:], 0.0))
+    v(V.memset(T.zf[:], 0.0))
     if r == 0:
         v(V.quantize_mx(T.wx[:, 8:136], T.swx[:, 8:136], T.zt[:]))
         vw()
@@ -232,73 +252,73 @@ def rank_program(g, core, T, topo):
     wait(V, "dw0")
     inc(V.quantize_mx(T.qw[:, 0:384], T.sw[:, 0:384], T.wt[:, 0:1536]), "ew")
     vw()
+    wait(V, "ec")
+    wait(V, "sk")
+    wait(V, "eza")
+    wait(V, "sk2")
 
     if r > 0:
         S.wait_ge(T.sem.msg, msg)
         inc(S.activation(T.jr[:, 0:r], T.mg[:, 0:r, 16], F.Copy, accum_out=T.cr[:]), "ecr")
-    V.wait_ge(T.sem.msg, msg)
+        wait(S, "ecr")
+        inc(S.activation(T.cr2[:], T.cr[:], F.Copy, bias=-256.0), "ecr2")
     wait(V, "so")
-    inc(V.tensor_tensor(T.pr[:, 0:112], T.mg[:, 0:N - 1, 17:33], T.mg[:, 1:N, 0:16], A.mult), "v")
+    V.wait_ge(T.sem.msg, msg)
     if r > 0:
-        v(V.tensor_tensor(T.po[:, 0:8], T.mg[:, r, 8:16], T.mg[:, r - 1, 25:33], A.mult))
+        inc(V.tensor_tensor(T.pa[:, 0:E], T.mg[:, 0:r, 17:25], T.mg[:, 1:r + 1, 0:8], A.mult), "vp")
+    if r > 1:
+        inc(V.tensor_tensor(T.za[:, 8:E], T.mg[:, 0:r - 1, 25:33], T.mg[:, 1:r, 8:16], A.mult), "vp")
+    if r > 0:
+        inc(V.tensor_tensor(T.po[:, 0:8], T.mg[:, r, 8:16], T.mg[:, r - 1, 25:33], A.mult), "vq")
     if r < N - 1:
-        v(V.tensor_tensor(T.po[:, 120:128], T.mg[:, r, 17:25], T.mg[:, r + 1, 0:8], A.mult))
-    vw()
+        inc(V.tensor_tensor(T.po[:, 120:128], T.mg[:, r, 17:25], T.mg[:, r + 1, 0:8], A.mult), "vq")
     if r > 0:
+        wait(V, "vp")
         wait(V, "ecr")
-    v(V.tensor_tensor_scan(T.cs[:], T.zt[:, 0:120], T.pr[:], T.cr[:] if r > 0 else 0.0, A.add, A.add))
+    inc(V.tensor_tensor_scan(T.cA[:, 0:E + 2], T.za[:, 0:E + 2], T.pa[:, 0:E + 2], T.cr[:] if r > 0 else 0.0,
+                             A.add, A.add), "va")
+    wait(V, "vq")
     inc(V.tensor_tensor_scan(T.rr[:], T.base[:], T.po[:], 0.0, A.add, A.add), "err")
-    wait(V, "sk")
-    wait(V, "sk2")
-    vw()
-    thr = T.c1
     if r > 0:
-        thr = T.thr
-        a8 = T.cs[:, 16 * r - 9:16 * r - 8]
-        v(V.tensor_scalar(T.tb[:], T.c63[:], a8, BIG, A.add, A.add))
-        v(V.tensor_scalar(T.tw[:], T.c1[:], a8, None, A.subtract))
-        vw()
-        inc(V.tensor_scalar(T.thr[:, 0:1], T.tb[:, 0:1], BIG, T.tw[:, 0:1], A.subtract, A.add), "eth")
-        v(V.tensor_scalar(T.thr[:, 1:2], T.tb[:, 1:2], BIG, T.tw[:, 1:2], A.subtract, A.add))
-        wait(S, "eth")
+        wait(V, "ecr2")
+    inc(V.tensor_tensor_scan(T.cB[:, 0:E + 2], T.za[:, 0:E + 2], T.pa[:, 0:E + 2], T.cr2[:] if r > 0 else -256.0,
+                             A.add, A.add), "vb")
+    wait(V, "va")
+    inc(V.tensor_scalar(T.thr[:], T.cA[:, E + 1:E + 2], T.cA[:, E - 1:E] if r > 0 else 0.0, None, A.subtract), "eth")
+    wait(V, "err")
+    wait(V, "vb")
+    v(V.tensor_scalar(T.cm[:], T.rr[:], T.cB[:, E - 1:E] if r > 0 else -256.0, T.cB[:, E + 1:E + 2], A.add, A.is_le))
     wait(S, "err")
-    wait(S, "sk2")
-    inc(S.activation(T.j3[:], T.rr[:], F.Sign, bias=thr[:, 0:1], scale=-1.0, accum_out=T.acl[:]), "sa")
+    wait(S, "eth")
+    inc(S.activation(T.j3[:], T.rr[:], F.Sign, bias=T.thr[:], scale=-1.0, accum_out=T.acl[:]), "sa")
     wait(S, "sa")
     inc(S.activation(T.it[:, 0:32], T.mh[:], F.Copy, scale=T.acl[:]), "et")
     vw()
-    wait(V, "err")
-    if r > 0:
-        wait(V, "eth")
-    v(V.tensor_scalar(T.cm[:], T.rr[:], thr[:, 1:2], 0.5, A.is_le, A.subtract))
+    v(V.tensor_tensor_scan(T.cn[:], T.cm[:], T.zt[:, 0:128], -64.0, A.add, A.add))
     vw()
-    v(V.tensor_reduce(T.cl1[:], T.cm[:], AxisListType.X, A.add))
-    vw()
-    wait(V, "ec")
-    v(V.tensor_scalar(T.it[:, 32:64], T.m1[:], T.cl1[:], None, A.mult))
-    vw()
+    v(V.tensor_scalar(T.it[:, 32:64], T.m1[:], T.cn[:, 127:128], None, A.mult))
     wait(V, "et")
+    vw()
     v(V.transpose(T.tt[:], T.it[:]))
     vw()
     v(V.tensor_tensor_scan(T.ss[:], T.rs[:], T.tt[:], 0.0, A.mult, A.add))
     vw()
     kk = [T.kk[:, 0:1], T.kk[:, 1:2], 352.0]
-    for b in (0, 1):
+    for k in range(3):
+        inc(V.tensor_scalar(T.off[:, k:24:3], T.ss[:, 7:64:8], 63.0, kk[k], A.min, A.add), "eo")
+    for q in (V, S):
+        q.wait_ge(T.sem.halo, halo)
+        wait(q, "eo")
+    for b, js in enumerate(BATCH):
         h = "ab"[b]
-        off, par = T["off" + h], (r + 1 + b) % 2
-        for k in range(3):
-            inc(V.tensor_scalar(off[:, k:12:3], T.ss[:, 7 + 8 * par:64:16], 63.0, kk[k], A.min, A.add), "eo" + h)
-        for q in (V, S):
-            wait(q, "eo" + h)
-            if b == 0:
-                q.wait_ge(T.sem.halo, halo)
-        inc(V.tensor_copy(T["slot" + h][:].bitcast(dt.uint32), T.wx[:].bitcast(dt.uint32).indirect(off[:])), "ep" + h)
-        inc(S.activation(T["sslot" + h][:], T.swx[:].indirect(off[:]), F.Copy), "es" + h)
+        off = T.off[:, 3 * js[0]:3 * js[0] + 3 * len(js)]
+        inc(V.tensor_copy(T["slot" + h][:].bitcast(dt.uint32), T.wx[:].bitcast(dt.uint32).indirect(off)), "ep" + h)
+        inc(S.activation(T["sslot" + h][:], T.swx[:].indirect(off), F.Copy), "es" + h)
         for plane in (0, 1):
             wait(g, ("es" if plane else "ep") + h)
             tr = []
-            for d, es in deal(r, b, plane).items():
-                i = 48 * (d // 2)
+            for i, (d, es) in enumerate(deal(r, b, plane).items()):
+                i = 48 * i
                 if plane:
                     src, dst = T["sslot" + h][:, i:i + 40], T.sland[:, 48 * r:48 * r + 40]
                 else:
@@ -309,12 +329,14 @@ def rank_program(g, core, T, topo):
             g.remote_dma_fused(tr, local_sem=T.sem.loc)
     cod = 0
     for s in others:
-        for b in (0, 1):
+        for b in range(len(BATCH)):
             for plane in (0, 1):
                 cod += len(deal(s, b, plane).get(r, []))
 
     for k in range(3):
-        inc(V.tensor_scalar(T.offo[:, k:k + 1], T.ss[:, 8 * r + 7:8 * r + 8], 63.0, kk[k], A.min, A.add), "eo2")
+        inc(V.tensor_scalar(T.offo[:, k:k + 1], T.ss[:, 8 * OWN + 7:8 * OWN + 8], 63.0, kk[k], A.min, A.add), "eo2")
+    v(V.tensor_tensor(T.pf[:, 0:56], T.mg[:, 0:N - 1, 17:25], T.mg[:, 1:N, 0:8], A.mult))
+    v(V.tensor_tensor(T.zf[:, 8:64], T.mg[:, 0:N - 1, 25:33], T.mg[:, 1:N, 8:16], A.mult))
     v(V.tensor_tensor_scan(T.cc[:], T.mg[:, :, 16], T.zt[:, 0:8], 0.0, A.add, A.add))
     wait(V, "gi3")
     v(V.tensor_scalar(T.kr[:], T.kr0[:], T.cf[:, 2:3], 0.125, A.add, A.mult))
@@ -322,13 +344,15 @@ def rank_program(g, core, T, topo):
         v(V.tensor_scalar(T.n2[:], T.n0[:], T.hs[:], T.cr[:], A.add, A.add))
     else:
         v(V.tensor_scalar(T.n2[:], T.n0[:], T.hs[:], None, A.add))
+    vw()
+    v(V.tensor_tensor_scan(T.cs[:], T.zf[:], T.pf[:], T.cr[:] if r > 0 else 0.0, A.add, A.add))
     wait(V, "eo2")
     inc(V.tensor_copy(T.land[:, 48 * r:48 * r + 48].bitcast(dt.uint32),
                       T.wx[:].bitcast(dt.uint32).indirect(T.offo[:, 0:3])), "ep2")
     wait(S, "eo2")
     inc(S.activation(T.sland[:, 48 * r:48 * r + 48], T.swx[:].indirect(T.offo[:, 0:3]), F.Copy), "es2")
     vw()
-    v(V.tensor_tensor(T.aq[:], T.cc[:], T.cs[:, 7:120:16], A.add))
+    v(V.tensor_tensor(T.aq[:], T.cc[:], T.cs[:, 7:64:8], A.add))
     v(V.quantize_mx(T.land[:, 384:512], T.sland[:, 384:512], T.zt[:]))
     v(V.quantize_mx(T.mv[:, 320:448], T.smv[:, 320:448], T.zt[:]))
     vw()
@@ -375,4 +399,4 @@ def rank_program(g, core, T, topo):
     wait(S, "ys")
     inc(S.dma_start(T.y[:, 64:128], T.yo[:, 64:128]), "dy", 16)
     wait(Y, "dy")
-    g.wait_ge(T.sem.loc, 7 * len(engs(others[0])))
+    g.wait_ge(T.sem.loc, (2 * len(BATCH) + len(near)) * len(engs(others[0])))

from concourse.bass import DstId, RemoteDMATransfer
from concourse.mybir import dt, AluOpType, AxisListType, ActivationFunctionType

A = AluOpType
F = ActivationFunctionType
C4, U8 = "float8_e4m3fn_x4", "uint8"
BF, F32 = "bfloat16", "float32"
BIG = 1.5 * 2.0 ** 32
ST = 40
W0 = 2560
BATCH = ((0, 1, 2), (4, 5, 6, 7))
OWN = 3
SCRATCH = {
    "xs": ("sbuf", [128, 512], BF), "us": ("sbuf", [128, 4], BF), "ut": ("sbuf", [128, 512], BF),
    "ln": ("sbuf", [128, 512], BF), "rn": ("sbuf", [128, 512], BF), "zt": ("sbuf", [128, 512], BF),
    "wt": ("sbuf", [128, 5120], BF),
    "qu": ("sbuf", [128, 128], C4), "su": ("sbuf", [128, 128], U8),
    "qx": ("sbuf", [128, 128], C4), "sx": ("sbuf", [128, 128], U8),
    "wx": ("sbuf", [128, 416], C4), "swx": ("sbuf", [128, 416], U8),
    "slota": ("sbuf", [128, 144], C4), "sslota": ("sbuf", [128, 144], U8),
    "slotb": ("sbuf", [128, 192], C4), "sslotb": ("sbuf", [128, 192], U8),
    "land": ("sbuf", [128, 512], C4), "sland": ("sbuf", [128, 512], U8),
    "mv": ("sbuf", [128, 448], C4), "smv": ("sbuf", [128, 448], U8),
    "qw": ("sbuf", [128, 1280], C4), "sw": ("sbuf", [128, 1280], U8),
    "sgp": ("sbuf", [128, 18, 10], BF), "nb": ("sbuf", [128, 640], BF), "ow": ("sbuf", [128, 640], BF),
    "a4": ("sbuf", [128, 640], BF), "nnp": ("sbuf", [128, 144], BF),
    "mo": ("sbuf", [128, ST * 128], BF), "mg": ("sbuf", [128, 8, 40], BF), "jr": ("sbuf", [128, 8], F32),
    "cr": ("sbuf", [128, 1], F32), "cr2": ("sbuf", [128, 1], F32), "j3": ("sbuf", [128, 128], F32),
    "base": ("sbuf", [128, 128], BF), "po": ("sbuf", [128, 128], BF),
    "pa": ("sbuf", [128, 64], BF), "za": ("sbuf", [128, 64], BF), "cA": ("sbuf", [128, 64], F32),
    "cB": ("sbuf", [128, 64], F32), "pf": ("sbuf", [128, 64], BF), "zf": ("sbuf", [128, 64], BF),
    "cc": ("sbuf", [128, 8], F32), "cs": ("sbuf", [128, 64], F32), "aq": ("sbuf", [128, 8], F32),
    "rr": ("sbuf", [128, 128], BF),
    "pi": ("sbuf", [128, 1], "int32"), "ci": ("sbuf", [128, 3], "int32"), "cf": ("sbuf", [128, 3], F32),
    "mi": ("sbuf", [128, 32], "int32"), "mj": ("sbuf", [128, 32], "int32"), "i2": ("sbuf", [128, 1], F32),
    "rs0": ("sbuf", [128, 64], F32), "rs": ("sbuf", [128, 64], F32),
    "c1": ("sbuf", [128, 1], F32), "mh": ("sbuf", [128, 32], F32),
    "m1": ("sbuf", [128, 32], F32), "kk": ("sbuf", [128, 2], F32), "hs": ("sbuf", [128, 1], F32),
    "thr": ("sbuf", [128, 1], F32),
    "cm": ("sbuf", [128, 128], BF), "acl": ("sbuf", [128, 1], F32), "cn": ("sbuf", [128, 128], BF),
    "it": ("sbuf", [128, 64], F32), "tt": ("sbuf", [128, 64], F32), "ss": ("sbuf", [128, 64], F32),
    "off": ("sbuf", [128, 24], "uint16"), "offo": ("sbuf", [128, 4], "uint16"),
    "n0": ("sbuf", [128, 4], F32), "n2": ("sbuf", [128, 4], F32),
    "kr0": ("sbuf", [128, 5], F32), "kr": ("sbuf", [128, 5], F32), "cq": ("sbuf", [128, 32], F32),
    "sq": ("sbuf", [128, 32], F32), "offr": ("sbuf", [128, 20], "uint16"),
    "yo": ("sbuf", [128, 128], F32),
    "sc": ("psum", [128, 512], F32), "ps": ("psum", [128, 1024], F32),
}
SEMAPHORES = ["v", "z", "du", "dx", "dl", "dw0", "dw1", "gi", "gi2", "gi3", "ect", "eut", "eu", "eq", "pm", "esg", "eow",
              "s1", "ea", "em", "so", "sz", "ec", "eza", "sk", "sk2", "ecr", "ecr2", "eth", "err", "sa", "et", "eo", "epa",
              "esa", "epb", "esb", "eo2", "ep2", "es2", "ew", "er", "py0", "py1", "yv", "ys", "dy", "vp", "vq", "va", "vb",
              "halo", "msg", "cod", "loc", "lm"] + ["kv%d" % k for k in range(5)] + ["ks%d" % k for k in range(5)]


def rank_program(g, core, T, topo):
    r = T.rank_of(core)
    if r is None:
        return
    N = len(T.cores)
    V, S, Y, P = g.vector, g.scalar, g.sync, g.tensor
    cnt = {}

    def inc(i, name, k=1):
        i.then_inc(T.sem[name], k)
        cnt[name] = cnt.get(name, 0) + k

    def wait(q, name):
        q.wait_ge(T.sem[name], cnt[name])

    def v(i):
        inc(i, "v")

    def vw():
        wait(V, "v")

    def to(d):
        rid, pnc = topo.addr(T.cores[d], core)
        return DstId(rid=rid, pnc=pnc)

    def engs(d, s=r):
        return topo.engines(T.cores[s], T.cores[d])

    def mask(es):
        return int(sum(1 << e for e in es))

    others = [(r + j) % N for j in range(1, N)]

    def nears(s):
        return [d for d in (s - 1, s + 1) if 0 <= d < N]

    near = nears(r)

    def deal(s, b, plane):
        ds = [(s + j - OWN) % N for j in BATCH[b]]
        es = engs(ds[0], s)
        n = len(es) // 4
        w = [1] * 4 if len(ds) == 4 else [2, 1, 1] if plane else [1, 1, 2]
        out, at = {}, 0
        for d, k in zip(ds, w):
            out[d] = es[at:at + n * k]
            at += n * k
        return out

    inc(S.dma_start(T.us[:], T.u[:, 0:4]), "du", 16)
    inc(Y.dma_start(T.xs[:], T.x[:]), "dx", 16)
    inc(S.dma_start(T.ln[:, 4:512], T.x[:, 0:508]), "dl", 16)
    inc(Y.dma_start(T.rn[:, 0:508], T.x[:, 4:512]), "dl", 16)
    inc(Y.dma_start(T.wt[:, 0:W0], T.w[:, 0:W0]), "dw0", 16)

    inc(g.iota(T.pi[:], [[1, 1]], 0, 8), "gi")
    inc(g.iota(T.mi[:], [[1, 32]], 256, -1), "gi")
    inc(g.iota(T.rs0[:], [[0, 8], [1, 8]], 0, 0, allow_small_or_imprecise_dtypes=True), "gi")
    inc(g.iota(T.i2[:], [[0, 1]], 4, 0, allow_small_or_imprecise_dtypes=True), "gi2")
    inc(V.memset(T.zt[:], 0.0), "z")
    v(V.memset(T.ow[:], 1.0))
    v(V.memset(T.sgp[:], 0.0))
    v(V.memset(T.nnp[:], 0.0))
    vw()
    v(V.memset(T.ow[:, 0:640:5], 0.0))

    wait(S, "z")
    inc(S.activation(T.nb[:, 4:640:5], T.zt[:, 0:128], F.Copy, bias=-1.0), "ect")
    wait(S, "ect")
    for a, b, st, k, c in ((9, 39, 5, 6, -0.75), (609, 639, 5, 6, -0.75), (44, 600, 40, 14, -0.75), (79, 600, 40, 14, -0.75),
                           (4, 40, 35, 2, -0.5), (604, 640, 35, 2, -0.5)):
        inc(S.activation(T.nb[:, a:b:st], T.zt[:, 0:k], F.Copy, bias=c), "ect")

    wait(S, "du")
    inc(S.activation(T.ut[:, 3:512:4], T.zt[:, 0:128], F.Identity, bias=T.us[:, 3:4]), "eut")
    wait(V, "z")
    wait(V, "du")
    for t in range(3):
        v(V.tensor_scalar(T.ut[:, t:512:4], T.zt[:, 0:128], T.us[:, t:t + 1], None, A.add))
    wait(V, "eut")
    vw()
    inc(V.quantize_mx(T.qu[:], T.su[:], T.ut[:]), "eu")
    wait(V, "dx")
    inc(V.quantize_mx(T.qx[:], T.sx[:], T.xs[:]), "eq")
    wait(P, "eu")
    wait(P, "eq")
    inc(P.matmul_mx(T.sc[:, 0:128], T.qu[:], T.su[:], T.qx[:], T.sx[:], True, True), "pm")

    def send_halo(plane, ds, sent):
        tr = []
        for i, d in enumerate(ds):
            a, b = (120, 8) if d > r else (0, 144)
            es = engs(d)
            n = len(es) // len(ds)
            if plane:
                src, dst = T.sx[:, a:a + 8], T.swx[:, b:b + 8]
            else:
                src, dst = T.qx[:, a:a + 8].bitcast(dt.uint8), T.wx[:, b:b + 8].bitcast(dt.uint8)
            tr.append(RemoteDMATransfer(dst_ids=[to(d)], dma_engine_mask=mask(es[n * i:n * i + n]), remote_sem=T.sem.halo,
                                        src=src, dst=dst))
        g.remote_dma_fused(tr, local_sem=T.sem[sent])

    wait(g, "eq")
    send_halo(1, near[:1], "lm")
    halo = sum(len(engs(r, d)) + len(engs(r, d)) // len(nears(d)) for d in near)

    wait(V, "pm")
    inc(V.tensor_scalar(T.sgp[:, 1:17, 1:9], T.sc[:, 0:128], -0.5, 0.5, A.max, A.min), "esg")
    n1 = 120 if 0 < r < N - 1 else 128
    b0 = ST * (n1 - 1)
    wait(S, "esg")
    inc(S.activation(T.ow[:, 4:640:5], T.sgp[:, 1:17, 1:9], F.Copy), "eow")
    if r > 0:
        inc(S.activation(T.mo[:, b0:b0 + 8], T.sgp[:, 1, 1:9], F.Copy, scale=4.0), "s1")
    if r < N - 1:
        inc(S.activation(T.mo[:, b0 + 25:b0 + 33], T.sgp[:, 16, 1:9], F.Copy, scale=4.0), "s1")
    wait(S, "dl")
    for t in range(4):
        inc(S.activation(T.ln[:, t:512:32], T.zt[:, 0:16], F.Copy), "sz")
        inc(S.activation(T.rn[:, 28 + t:512:32], T.zt[:, 0:16], F.Copy), "sz")
    wait(V, "esg")
    for k, (a, b) in enumerate(((1, 2), (1, 0), (2, 1), (0, 1))):
        v(V.tensor_scalar(T.nb[:, k:640:5], T.sgp[:, a:a + 16, b:b + 8], 1.0, None, A.mult))
    wait(V, "ect")
    wait(V, "eow")
    vw()
    inc(V.tensor_tensor_scan(T.a4[:], T.ow[:], T.nb[:], 0.0, A.mult, A.add), "ea")
    wait(V, "ea")
    v(V.tensor_scalar(T.nnp[:, 8:136], T.a4[:, 4:640:5], 0.0, -4.0, A.is_ge, A.mult))
    wait(V, "s1")
    vw()
    d0, d1 = (8, 0) if r == 0 else (8, 16)
    inc(V.tensor_tensor_scan(T.mo[:, 16:b0 + 17:ST], T.nnp[:, d0:d0 + n1], T.nnp[:, d1:d1 + n1], 1024.0,
                             A.add, A.add), "em")
    if r > 0:
        inc(V.tensor_tensor(T.mo[:, b0 + 8:b0 + 16], T.nnp[:, 8:16], T.sgp[:, 1, 1:9], A.mult), "em")
    if r < N - 1:
        inc(V.tensor_tensor(T.mo[:, b0 + 17:b0 + 25], T.nnp[:, 128:136], T.sgp[:, 16, 1:9], A.mult), "em")
    m0, m1 = (16 if r == 0 else 0), (17 if r == N - 1 else 33)
    wait(g, "em")
    wait(g, "s1")
    g.remote_dma_fused([RemoteDMATransfer(dst_ids=[to(d) for d in others], dma_engine_mask=mask(engs(others[0])),
                                          remote_sem=T.sem.msg, srcs=[T.mo[:, b0 + m0:b0 + m1]],
                                          dsts=[T.mg[:, r, m0:m1] for d in others])], local_sem=T.sem.lm)
    send_halo(0, near, "loc")
    Y.wait_ge(T.sem.lm, 2 * len(engs(others[0])))
    inc(Y.dma_start(T.wt[:, W0:5120], T.w[:, W0:5120]), "dw1", 16)
    if near[1:]:
        send_halo(1, near[1:], "loc")
    inc(g.iota(T.n0[:], [[1024, 4]], 64 * r, 0, allow_small_or_imprecise_dtypes=True), "gi3")
    inc(g.iota(T.kr0[:], [[64, 5]], 0, 0, allow_small_or_imprecise_dtypes=True), "gi3")
    msg = sum(len(engs(r, d)) for d in others)
    wait(S, "em")
    wait(S, "s1")
    inc(S.activation(T.mg[:, r, m0:m1], T.mo[:, b0 + m0:b0 + m1], F.Copy), "so")

    E = 8 * r
    wait(V, "gi")
    v(V.tensor_scalar(T.ci[:, 0:1], T.pi[:], 248, None, A.bitwise_and))
    v(V.tensor_scalar(T.ci[:, 1:2], T.pi[:], 64, None, A.bitwise_and))
    v(V.tensor_scalar(T.ci[:, 2:3], T.pi[:], 56, None, A.bitwise_and))
    v(V.tensor_scalar(T.mj[:], T.mi[:], 7, None, A.bitwise_and))
    v(V.tensor_scalar(T.rs[:], T.rs0[:], 0.5, None, A.is_gt))
    if r > 0:
        inc(V.memset(T.za[:, 0:E], 0.0), "eza")
    inc(V.memset(T.za[:, E + 1:E + 2], -BIG), "eza")
    inc(V.memset(T.pa[:, E:E + 1], BIG), "eza")
    vw()
    inc(V.tensor_copy(T.cf[:], T.ci[:]), "ec")
    inc(V.tensor_scalar(T.m1[:], T.mj[:], 0.0, None, A.is_equal), "ec")
    wait(S, "ec")
    wait(S, "gi2")
    inc(S.activation(T.c1[:], T.i2[:], F.Identity, bias=T.cf[:, 0:1]), "sk")
    inc(S.activation(T.kk[:, 0:1], T.cf[:, 1:2], F.Copy, bias=80.0, scale=-0.125), "sk")
    inc(S.activation(T.kk[:, 1:2], T.cf[:, 1:2], F.Copy, bias=88.0, scale=2.125), "sk")
    inc(S.activation(T.hs[:], T.cf[:, 1:2], F.Identity, bias=T.cf[:, 2:3], scale=8.0), "sk")
    inc(S.activation(T.mh[:], T.m1[:], F.Copy, scale=0.5), "sk")
    wait(S, "sk")
    sh = 64 * ((r - OWN) % N)
    inc(S.activation(T.za[:, E:E + 1], T.c1[:], F.Copy, bias=256.0 - sh, scale=-1.0), "sk2")
    inc(S.activation(T.pa[:, E + 1:E + 2], T.c1[:], F.Copy, bias=float(sh)), "sk2")
    v(V.tensor_scalar(T.base[:, 8:120], T.nnp[:, 16:128], 2.0, 8.0, A.mult, A.add))
    v(V.tensor_scalar(T.base[:, 0:8], T.nnp[:, 8:16], 1.0 if r > 0 else 2.0, 8.0, A.mult, A.add))
    v(V.tensor_scalar(T.base[:, 120:128], T.nnp[:, 128:136], 1.0 if r < N - 1 else 2.0, 8.0, A.mult, A.add))
    v(V.memset(T.po[:], 0.0))
    v(V.memset(T.pf[:], 0.0))
    v(V.memset(T.zf[:], 0.0))
    if r == 0:
        v(V.quantize_mx(T.wx[:, 8:136], T.swx[:, 8:136], T.zt[:]))
        vw()
    if r == N - 1:
        v(V.quantize_mx(T.wx[:, 24:152], T.swx[:, 24:152], T.zt[:]))
        vw()
    v(V.quantize_mx(T.wx[:, 16:144], T.swx[:, 16:144], T.xs[:]))
    wait(V, "sz")
    v(V.quantize_mx(T.wx[:, 160:288], T.swx[:, 160:288], T.ln[:]))
    v(V.quantize_mx(T.wx[:, 288:416], T.swx[:, 288:416], T.rn[:]))
    wait(V, "dw0")
    inc(V.quantize_mx(T.qw[:, 0:384], T.sw[:, 0:384], T.wt[:, 0:1536]), "ew")
    vw()
    wait(V, "ec")
    wait(V, "sk")
    wait(V, "eza")
    wait(V, "sk2")

    if r > 0:
        S.wait_ge(T.sem.msg, msg)
        inc(S.activation(T.jr[:, 0:r], T.mg[:, 0:r, 16], F.Copy, accum_out=T.cr[:]), "ecr")
        wait(S, "ecr")
        inc(S.activation(T.cr2[:], T.cr[:], F.Copy, bias=-256.0), "ecr2")
    wait(V, "so")
    V.wait_ge(T.sem.msg, msg)
    if r > 0:
        inc(V.tensor_tensor(T.pa[:, 0:E], T.mg[:, 0:r, 17:25], T.mg[:, 1:r + 1, 0:8], A.mult), "vp")
    if r > 1:
        inc(V.tensor_tensor(T.za[:, 8:E], T.mg[:, 0:r - 1, 25:33], T.mg[:, 1:r, 8:16], A.mult), "vp")
    if r > 0:
        inc(V.tensor_tensor(T.po[:, 0:8], T.mg[:, r, 8:16], T.mg[:, r - 1, 25:33], A.mult), "vq")
    if r < N - 1:
        inc(V.tensor_tensor(T.po[:, 120:128], T.mg[:, r, 17:25], T.mg[:, r + 1, 0:8], A.mult), "vq")
    if r > 0:
        wait(V, "vp")
        wait(V, "ecr")
    inc(V.tensor_tensor_scan(T.cA[:, 0:E + 2], T.za[:, 0:E + 2], T.pa[:, 0:E + 2], T.cr[:] if r > 0 else 0.0,
                             A.add, A.add), "va")
    wait(V, "vq")
    inc(V.tensor_tensor_scan(T.rr[:], T.base[:], T.po[:], 0.0, A.add, A.add), "err")
    if r > 0:
        wait(V, "ecr2")
    inc(V.tensor_tensor_scan(T.cB[:, 0:E + 2], T.za[:, 0:E + 2], T.pa[:, 0:E + 2], T.cr2[:] if r > 0 else -256.0,
                             A.add, A.add), "vb")
    wait(V, "va")
    inc(V.tensor_scalar(T.thr[:], T.cA[:, E + 1:E + 2], T.cA[:, E - 1:E] if r > 0 else 0.0, None, A.subtract), "eth")
    wait(V, "err")
    wait(V, "vb")
    v(V.tensor_scalar(T.cm[:], T.rr[:], T.cB[:, E - 1:E] if r > 0 else -256.0, T.cB[:, E + 1:E + 2], A.add, A.is_le))
    wait(S, "err")
    wait(S, "eth")
    inc(S.activation(T.j3[:], T.rr[:], F.Sign, bias=T.thr[:], scale=-1.0, accum_out=T.acl[:]), "sa")
    wait(S, "sa")
    inc(S.activation(T.it[:, 0:32], T.mh[:], F.Copy, scale=T.acl[:]), "et")
    vw()
    v(V.tensor_tensor_scan(T.cn[:], T.cm[:], T.zt[:, 0:128], -64.0, A.add, A.add))
    vw()
    v(V.tensor_scalar(T.it[:, 32:64], T.m1[:], T.cn[:, 127:128], None, A.mult))
    wait(V, "et")
    vw()
    v(V.transpose(T.tt[:], T.it[:]))
    vw()
    v(V.tensor_tensor_scan(T.ss[:], T.rs[:], T.tt[:], 0.0, A.mult, A.add))
    vw()
    kk = [T.kk[:, 0:1], T.kk[:, 1:2], 352.0]
    for k in range(3):
        inc(V.tensor_scalar(T.off[:, k:24:3], T.ss[:, 7:64:8], 63.0, kk[k], A.min, A.add), "eo")
    for q in (V, S):
        q.wait_ge(T.sem.halo, halo)
        wait(q, "eo")
    for b, js in enumerate(BATCH):
        h = "ab"[b]
        off = T.off[:, 3 * js[0]:3 * js[0] + 3 * len(js)]
        inc(V.tensor_copy(T["slot" + h][:].bitcast(dt.uint32), T.wx[:].bitcast(dt.uint32).indirect(off)), "ep" + h)
        inc(S.activation(T["sslot" + h][:], T.swx[:].indirect(off), F.Copy), "es" + h)
        for plane in (0, 1):
            wait(g, ("es" if plane else "ep") + h)
            tr = []
            for i, (d, es) in enumerate(deal(r, b, plane).items()):
                i = 48 * i
                if plane:
                    src, dst = T["sslot" + h][:, i:i + 40], T.sland[:, 48 * r:48 * r + 40]
                else:
                    src = T["slot" + h][:, i:i + 40].bitcast(dt.uint8)
                    dst = T.land[:, 48 * r:48 * r + 40].bitcast(dt.uint8)
                tr.append(RemoteDMATransfer(dst_ids=[to(d)], dma_engine_mask=mask(es), remote_sem=T.sem.cod,
                                            src=src, dst=dst))
            g.remote_dma_fused(tr, local_sem=T.sem.loc)
    cod = 0
    for s in others:
        for b in range(len(BATCH)):
            for plane in (0, 1):
                cod += len(deal(s, b, plane).get(r, []))

    for k in range(3):
        inc(V.tensor_scalar(T.offo[:, k:k + 1], T.ss[:, 8 * OWN + 7:8 * OWN + 8], 63.0, kk[k], A.min, A.add), "eo2")
    v(V.tensor_tensor(T.pf[:, 0:56], T.mg[:, 0:N - 1, 17:25], T.mg[:, 1:N, 0:8], A.mult))
    v(V.tensor_tensor(T.zf[:, 8:64], T.mg[:, 0:N - 1, 25:33], T.mg[:, 1:N, 8:16], A.mult))
    v(V.tensor_tensor_scan(T.cc[:], T.mg[:, :, 16], T.zt[:, 0:8], 0.0, A.add, A.add))
    wait(V, "gi3")
    v(V.tensor_scalar(T.kr[:], T.kr0[:], T.cf[:, 2:3], 0.125, A.add, A.mult))
    if r > 0:
        v(V.tensor_scalar(T.n2[:], T.n0[:], T.hs[:], T.cr[:], A.add, A.add))
    else:
        v(V.tensor_scalar(T.n2[:], T.n0[:], T.hs[:], None, A.add))
    vw()
    v(V.tensor_tensor_scan(T.cs[:], T.zf[:], T.pf[:], T.cr[:] if r > 0 else 0.0, A.add, A.add))
    wait(V, "eo2")
    inc(V.tensor_copy(T.land[:, 48 * r:48 * r + 48].bitcast(dt.uint32),
                      T.wx[:].bitcast(dt.uint32).indirect(T.offo[:, 0:3])), "ep2")
    wait(S, "eo2")
    inc(S.activation(T.sland[:, 48 * r:48 * r + 48], T.swx[:].indirect(T.offo[:, 0:3]), F.Copy), "es2")
    vw()
    v(V.tensor_tensor(T.aq[:], T.cc[:], T.cs[:, 7:64:8], A.add))
    v(V.quantize_mx(T.land[:, 384:512], T.sland[:, 384:512], T.zt[:]))
    v(V.quantize_mx(T.mv[:, 320:448], T.smv[:, 320:448], T.zt[:]))
    vw()
    for c in range(4):
        v(V.tensor_scalar(T.cq[:, 8 * c:8 * c + 8], T.aq[:], T.n2[:, c:c + 1], 48.0, A.is_le, A.mult))
    vw()
    v(V.tensor_tensor_scan(T.sq[:], T.rs[:, 0:32], T.cq[:], 0.0, A.mult, A.add))
    vw()
    for k in range(5):
        inc(V.tensor_scalar(T.offr[:, 4 * k:4 * k + 4], T.sq[:, 7:32:8], T.kr[:, k:k + 1], None, A.add), "er")

    wait(V, "dw1")
    inc(V.quantize_mx(T.qw[:, 384:896], T.sw[:, 384:896], T.wt[:, 1536:3584]), "ew")
    inc(V.quantize_mx(T.qw[:, 896:1280], T.sw[:, 896:1280], T.wt[:, 3584:5120]), "ew")
    vw()

    for q in (V, S):
        wait(q, "er")
        wait(q, "ep2")
        wait(q, "es2")
        q.wait_ge(T.sem.cod, cod)
    wait(P, "ew")
    for k in range(5):
        o16, at = T.offr[:, 4 * k:4 * k + 4], 64 * (4 - k)
        inc(V.tensor_copy(T.mv[:, at:at + 64].bitcast(dt.uint32),
                          T.land[:].bitcast(dt.uint32).indirect(o16)), "kv%d" % k)
        inc(S.activation(T.smv[:, at:at + 64], T.sland[:].indirect(o16), F.Copy), "ks%d" % k)
    for k in range(5):
        at = 64 * (4 - k)
        wait(P, "kv%d" % k)
        wait(P, "ks%d" % k)
        for o in (0, 1):
            w0 = 128 * (2 * k + o)
            i = P.matmul_mx(T.ps[:, 512 * o:512 * o + 128], T.qw[:, w0:w0 + 128], T.sw[:, w0:w0 + 128],
                            T.mv[:, at:at + 128], T.smv[:, at:at + 128], k == 0, k == 4)
            if k == 4:
                inc(i, "py%d" % o)
    wait(V, "py0")
    inc(V.tensor_copy(T.yo[:, 0:64], T.ps[:, 0:64]), "yv")
    wait(Y, "yv")
    inc(Y.dma_start(T.y[:, 0:64], T.yo[:, 0:64]), "dy", 16)
    wait(S, "py1")
    inc(S.activation(T.yo[:, 64:128], T.ps[:, 512:576], F.Copy), "ys")
    wait(S, "ys")
    inc(S.dma_start(T.y[:, 64:128], T.yo[:, 64:128]), "dy", 16)
    wait(Y, "dy")
    g.wait_ge(T.sem.loc, (2 * len(BATCH) + len(near)) * len(engs(others[0])))
